import numpy as np, ml_dtypes
CORES = [1,5,17,21,33,37,49,53]
N = 8
import mx_ref
BF = ml_dtypes.bfloat16
def pick(q, e):
    c = np.concatenate([q[0].reshape(128, -1, 4), np.zeros((128, 1, 4), np.uint8)], axis=1); s = np.concatenate([q[1], np.ones((16, 1), np.uint8)], axis=1)
    return (np.ascontiguousarray(c[:, e].reshape(128, -1)), np.ascontiguousarray(s[:, e]))
def join(*qs):
    return (np.concatenate([q[0] for q in qs], axis=1), np.concatenate([q[1] for q in qs], axis=1))
def put(q, e, v):
    c, s = q[0].reshape(128, -1, 4).copy(), q[1].copy(); c[:, e] = v[0].reshape(128, -1, 4); s[:, e] = v[1]
    return (c.reshape(128, -1), s)
def pk(c, s):
    return (np.ascontiguousarray(c), mx_ref.live(s))
def emit(q):
    return q[0], q[1]
def decode(q):
    o = []
    for b in range(4):
        e = np.zeros((128, 128, 4), np.float32); e[np.arange(128), np.arange(128), b] = 1
        o.append(mx_ref.matmul(mx_ref.quantize(e.reshape(128, 512).astype(BF)), q))
    return np.stack(o, axis=2).reshape(128, -1)
def f(rng, *shape):
    return mx_ref.flush((rng.standard_normal(shape, dtype=np.float32) * np.exp2(rng.integers(-2, 3, shape[:-1] + (1,)))).astype(BF))
def wide(rng, *shape, cols=0):
    v = rng.standard_normal(shape, dtype=np.float32) * np.exp2(rng.integers(-12, 13, shape)).astype(np.float32)
    if cols: v *= np.repeat(np.exp2(rng.integers(-cols, cols + 1, shape[:-2] + (1, shape[-1] // 4))) * (rng.random(shape[:-2] + (1, shape[-1] // 4)) > 0.0625), 4, axis=-1).astype(np.float32)
    return mx_ref.flush(v.astype(BF))
P, C, G, H = 64, 192, 16, 4
F = 96
def trim(v):
    v = v.astype(np.float32)
    v[np.abs(v) < np.float32(2.0 ** -20)] = 0
    return v.astype(BF)
def alike(v):
    return np.stack([v] * N).astype(np.float32).astype(BF)
def flat(v):
    return v.reshape(N, 128, -1).astype(np.float32).astype(BF)
def planted(rng, sign, m, a, b):
    v, t = 1 + rng.random((N, 128, P, 4)), 1 + rng.random((N, 128, C, 4))
    if sign < 0:
        v = 64.0 * (1 + (np.argsort(v, axis=-1) < 2))
        t[:] = 4
    for r in range(N):
        if sign < 0: v[r, m[r], np.arange(P)] = 128
        else: v[r, m[r], np.arange(P)] *= 64
        at = rng.permutation(np.arange(C) % F)
        g = np.zeros(C)
        if sign > 0:
            g[:] = 4
            o = rng.permutation(C)
            g[o[np.unique(at[o], return_index=True)[1]]] = 16
        t[r, at, np.arange(C)] *= g[:, None]
        t[r, :F] *= 2.0 ** 25 if sign < 0 else 2.0 ** 20
        t[r, F:] = 0
        t[r, F + 16:] = -b[r, at][None, :, None] * 2.0 ** 24
    v *= sign * 2.0 ** 20
    v[:, F:] = 0
    v[:, F:F + 16] = -a[:, None, :, None] * 2.0 ** 24
    u = np.zeros((128, 4))
    u[F:] = 2.0 ** 29
    return {"pn": flat(v), "x": flat(t), "u": alike(u), "w": f(rng, N, 128, 512)}
def setup_inputs(rng):
    return {"pn": trim(f(rng, N, 128, 4 * P)), "x": trim(f(rng, N, 128, 4 * C)), "u": alike(f(rng, 128, 4)), "w": f(rng, N, 128, 512)}
def setup_inputs_near(rng):
    K = min(P, C // 2)
    z = rng.integers(4, 8, (128, K, 4)) * rng.choice([-1.0, 1.0], (128, K, 4))
    z[:16] = 0
    u = rng.integers(4, 8, (128, 4)) * rng.choice([-1.0, 1.0], (128, 4))
    u[:16] = 0
    u[8, 0] = 2.0 ** -8
    v, t = np.zeros((N, 128, P, 4)), np.zeros((N, 128, C, 4))
    for r in range(N):
        v[r] = z[:, rng.permutation(np.arange(P) % K)]
        v[r, 0, :, 0] = 2.0 ** -4
        at = rng.permutation(np.arange(C) % K)
        small = np.ones(C)
        for k in range(K):
            e = np.flatnonzero(at == k)
            if k % 3 == 0: small[e[-1]] = 2
            if k % 3 == 2: small[e[0]] = 2
        more = np.full(K, -1.0)
        o = rng.permutation(K)
        more[o[:K // 2]] = 1
        more[o[K // 2:K // 2 + K // 4]] = 0
        t[r] = z[:, at]
        t[r, 0, :, 0] = small * 2.0 ** -4
        t[r, 8, :, 0] = more[at] * 2.0 ** -4
    g = 2.0 ** -int(rng.integers(12, 17))
    return {"pn": flat(v * g), "x": flat(t * g), "u": alike(u * 2.0 ** -int(rng.integers(12, 21))), "w": f(rng, N, 128, 512)}
def setup_inputs_below(rng):
    m, b = np.stack([rng.permutation(F)[:P] for r in range(N)]), np.full((N, F), 4.0)
    for r in range(N): b[(r + 1) % N, m[r, rng.permutation(P)[:2 * G]]] = 1
    return planted(rng, -1, m, np.full((N, P), 2.0), b)
def setup_inputs_crowd(rng):
    E = P // 2
    n = rng.permutation(np.array([G, 0, G + 1, G - 1, 1, E, G, G + 1])[:N])
    m, a = np.zeros((N, P), int), np.full((N, P), 8.0)
    for r in range(N):
        g = rng.permutation(np.arange(P) % E)
        m[r] = rng.permutation(F)[g]
        a[r, np.unique(g, return_index=True)[1][rng.permutation(E)[n[r]:]]] = 2
    return planted(rng, 1, m, a, np.full((N, F), 4.0))
def setup_inputs_spread(rng):
    return {**setup_inputs(rng), "pn": trim(wide(rng, N, 128, 4 * P, cols=6)), "x": trim(wide(rng, N, 128, 4 * C, cols=6))}
def check_inputs(d):
    b = []
    for k, lo, hi in (("pn", -20, 27), ("x", -20, 27), ("u", -30, 30), ("w", -30, 30)):
        v = np.abs(d[k].astype(np.float32))
        if not (np.isfinite(v).all() and ((v == 0) | (v >= 2.0 ** lo) & (v <= 2.0 ** hi)).all()): b.append("a value of " + k)
    v = d["u"].astype(np.float32)
    if not (v == v[:1]).all(): b.append("u differs between ranks")
    return b
def upto(e, n):
    return np.concatenate([e, np.full(n - len(e), -1)])
def visit(a, b, k):
    s = mx_ref.matmul(pick(a, upto(np.arange(P), 128)), b)[:P] + np.float32(0)
    place = np.argmax(s, axis=1)
    v = mx_ref.matmul(k, join(a, b))[0] + np.float32(0)
    owns = np.zeros(P, bool)
    owns[np.unique(place, return_index=True)[1]] = True
    i = np.flatnonzero(owns & (v[P + place] > v[:P]))[:G]
    if len(i) == 0: return a, b
    j = place[i]
    d = decode(join(pick(a, upto(i, G)), pick(b, upto(j, G))))
    z = mx_ref.quantize(np.ascontiguousarray((d[:, :4 * G] - np.float32(0.5) * d[:, 4 * G:]).astype(BF)))
    return put(a, i, pick(b, j)), put(b, j, pick(z, np.arange(len(i))))
def reference(pn, x, u, w):
    a = [mx_ref.quantize(np.ascontiguousarray(pn[r])) for r in range(N)]
    b = [mx_ref.quantize(np.ascontiguousarray(x[r])) for r in range(N)]
    k = [mx_ref.quantize(np.concatenate([u[r], np.zeros((128, 508), BF)], axis=1)) for r in range(N)]
    wq = [mx_ref.quantize(np.ascontiguousarray(w[r])) for r in range(N)]
    y = np.zeros((N, 128, H * P), np.float32)
    for h in range(H):
        a = [a[r - 1] for r in range(N)]
        for r in range(N):
            a[r], b[r] = visit(a[r], b[r], k[r])
            y[r, :, h * P:h * P + P] = mx_ref.matmul(wq[r], a[r])
    p, t = [emit(v) for v in a], [emit(v) for v in b]
    return {"y": y, "pc": np.stack([v[0] for v in p]), "psc": np.stack([v[1] for v in p]), "oc": np.stack([v[0] for v in t]), "osc": np.stack([v[1] for v in t])}

@@ -1,0 +1,300 @@
+from concourse.bass import DstId, RemoteDMATransfer
+from concourse.mybir import dt, AluOpType as A, AxisListType, ActivationFunctionType as F
+
+P, C, H = 64, 192, 4
+BIG = 1.0e6
+M4 = 1.5 * 2.0 ** 25
+M128 = 1.5 * 2.0 ** 30
+F32, BF16, I32, U16, F8, U8 = "float32", "bfloat16", "int32", "uint16", "float8_e4m3fn_x4", "uint8"
+
+SCRATCH = {}
+
+
+def _sb(dtype, **shapes):
+    for name in shapes:
+        SCRATCH[name] = ("sbuf", list(shapes[name]), dtype)
+
+
+_sb(BF16, tp=(128, 512), tx=(128, 768), tw=(128, 512), tu=(128, 4), ur=(128, 512), z0=(128, 512), wide1=(128, 516), wide2=(128, 516),
+    kt=(128, 512), xt=(128, 512), zt=(128, 512), vals=(128, P), sgn=(64, C), lt=(64, C), ne=(64, 64))
+_sb(F32, ones=(128, 128), zero=(64, C), i1=(128, 128), i2=(64, 64), k1=(64, 64), k2=(64, 64), i4=(32, 32), tri=(64, 32), i5=(64, 4),
+    m4a=(64, 4), m4b=(64, 4), mask4=(64, 4), islot=(128, 4), dcol=(128, 1), s1=(128, C), s2=(128, C), seg=(128, C), idx=(64, C),
+    maskb=(64, 16), ucol=(64, 1), cc=(64, 200), rr=(64, C), vs=(64, C), tc=(64, 1), hb=(64, 1), own=(64, 1), bx=(64, 64), by=(64, 64),
+    mm=(128, 4), scn=(128, C), ys=(128, H * P))
+_sb(I32, i3=(128, 16), i3b=(128, 16), i6=(128, 4), i6b=(128, 4), i7=(128, 4), i8=(128, C), i8b=(128, C))
+_sb(F8, urq=(128, 128), wq=(128, 128), kq=(128, 128), xq=(128, 128))
+_sb(U8, urs=(128, 128), ws=(128, 128), ks=(128, 128), xs=(128, 128))
+for _h in range(1, H + 2):
+    _sb(F8, **{"w%d" % _h: (128, 384)})
+    _sb(U8, **{"v%d" % _h: (128, 384)})
+for _h in range(H + 1):
+    _sb(F8, **{"p%d" % _h: (128, 192)})
+    _sb(U8, **{"q%d" % _h: (128, 192)})
+for _h in range(1, H + 1):
+    _sb(U16, **{"off%d" % _h: (128, 4), "tof%d" % _h: (128, 12)})
+    _sb(BF16, **{"win%d" % _h: (128, 256)})
+for _b in range(4):
+    _sb(F8, **{"eq%d" % _b: (128, 128), "nq%d" % _b: (128, 128)})
+    _sb(U8, **{"es%d" % _b: (128, 128), "ns%d" % _b: (128, 128)})
+for _n in ("psc_", "pur", "puc", "pk", "pd0", "pd1", "pd2", "pd3"):
+    SCRATCH[_n] = ("psum", [128, 512], F32)
+
+SEMAPHORES = ["cV", "cP", "cS", "cG", "lp", "lx", "lu", "lw", "fin"]
+SEMAPHORES += ["arr%d" % h for h in range(1, H + 1)] + ["snt%d" % h for h in range(H)] + ["st%d" % h for h in range(1, H + 1)]
+
+
+def rank_program(g, core, T, topo):
+    rank = T.rank_of(core)
+    if rank is None:
+        return
+    n = len(T.cores)
+    nxt, prv = T.cores[(rank + 1) % n], T.cores[(rank - 1) % n]
+
+    def lanes(a, b):
+        return topo.engines(a, b)[:8]
+
+    queue = {"V": g.vector, "P": g.tensor, "S": g.scalar, "G": g, "Y": g.sync}
+    cnt = {"V": 0, "P": 0, "S": 0, "G": 0}
+    known = {e: {} for e in queue}
+    res = {}
+    last = {}
+
+    def need(e, dep):
+        sem, val, clock = dep
+        if known[e].get(sem, 0) >= val:
+            return
+        queue[e].wait_ge(T.sem[sem], val)
+        known[e][sem] = val
+        for k, v in clock.items():
+            if known[e].get(k, 0) < v:
+                known[e][k] = v
+
+    def before(e, reads, writes, nowaw):
+        deps = []
+        for r in reads:
+            if r in res and res[r]["w"]: deps.append(res[r]["w"])
+        for w in writes:
+            if w in res:
+                if res[w]["w"] and not nowaw: deps.append(res[w]["w"])
+                deps += [d for (f, d) in res[w]["r"] if f != e]
+        for d in sorted(deps, key=lambda d: -d[1]):
+            need(e, d)
+
+    def after(e, reads, writes, dep):
+        for r in reads:
+            res.setdefault(r, {"w": None, "r": []})["r"].append((e, dep))
+        for w in writes:
+            res[w] = {"w": dep, "r": []}
+
+    def op(e, call, reads, writes, nowaw=False):
+        before(e, reads, writes, nowaw)
+        i = call()
+        cnt[e] += 1
+        sem = "c" + e
+        i.then_inc(T.sem[sem], 1)
+        last[sem] = cnt[e]
+        after(e, reads, writes, (sem, cnt[e], dict(known[e])))
+
+    def dma(e, out, in_, sem, reads, writes):
+        before(e, reads, writes, False)
+        queue[e].dma_start(out, in_).then_inc(T.sem[sem], 16)
+        last[sem] = last.get(sem, 0) + 16
+        after(e, reads, writes, (sem, last[sem], dict(known[e])))
+
+    V, PE, S = g.vector, g.tensor, g.scalar
+
+    def mset(ap, c, w):
+        op("V", lambda: V.memset(ap, c), [], [w])
+
+    def ts(out, in0, a, b, o0, o1, reads, writes):
+        if b is None:
+            op("V", lambda: V.tensor_scalar(out, in0, a, None, o0), reads, writes)
+        else:
+            op("V", lambda: V.tensor_scalar(out, in0, a, b, o0, o1), reads, writes)
+
+    def tt(out, a, b, o, reads, writes):
+        op("V", lambda: V.tensor_tensor(out, a, b, o), reads, writes)
+
+    def quant(q, s, t, reads, writes):
+        op("V", lambda: V.quantize_mx(q, s, t), reads, writes)
+
+    def mm(out, l, ls, r, rs, reads, writes, start=True, stop=True):
+        op("P", lambda: PE.matmul_mx(out, l, ls, r, rs, start, stop), reads, writes, nowaw=not start)
+
+    def act(out, in_, f, reads, writes, **kw):
+        op("S", lambda: S.activation(out, in_, f, **kw), reads, writes)
+
+    def iota(out, pat, base, cm, w, flag=True):
+        if flag:
+            op("G", lambda: g.iota(out, pat, base, cm, allow_small_or_imprecise_dtypes=True), [], [w])
+        else:
+            op("G", lambda: g.iota(out, pat, base, cm), [], [w])
+
+    def send(h):
+        rid, pid = topo.addr(nxt)[:2]
+        es = lanes(core, nxt)
+        mask = sum(1 << e for e in es)
+        arr, snt = T.sem["arr%d" % (h + 1)], T.sem["snt%d" % h]
+        before("G", ["p%d" % h], [], False)
+        g.remote_dma(out_ap=T["w%d" % (h + 1)][:, 0:P].bitcast(dt.uint8), in_ap=T["p%d" % h][:, 0:P].bitcast(dt.uint8),
+                     remote_sem=arr, local_sem=snt, pid=pid, routing_id=rid, dma_engine_mask=mask)
+        before("G", ["q%d" % h], [], False)
+        g.remote_dma(out_ap=T["v%d" % (h + 1)][:, 0:P], in_ap=T["q%d" % h][:, 0:P],
+                     remote_sem=arr, local_sem=snt, pid=pid, routing_id=rid, dma_engine_mask=mask)
+        last["snt%d" % h] = 2 * len(es)
+
+    dma("Y", T.tp[:, 0:256], T.pn[:], "lp", [], ["tp"])
+    dma("S", T.tx[:], T.x[:], "lx", [], ["tx"])
+    dma("Y", T.tu[:], T.u[:], "lu", [], ["tu"])
+    dma("Y", T.tw[:], T.w[:], "lw", [], ["tw"])
+
+    iota(T.i2[:], [[1, 16], [16, 4]], 0, -1, "i2")
+    iota(T.i3[:], [[1, 16]], 0, -1, "i3", False)
+    iota(T.i4[:], [[1, 32]], 0, -1, "i4")
+    iota(T.i5[:], [[-16, 4]], 0, 1, "i5")
+    iota(T.i6[:], [[0, 4]], 0, 1, "i6", False)
+    iota(T.i7[:], [[16, 4]], 0, 0, "i7", False)
+    iota(T.idx[:], [[8, C]], 68, 0, "idx")
+
+    mset(T.tp[:, 256:512], 0.0, "tpz")
+    mset(T.ones[:], 1.0, "ones")
+    mset(T.zero[:], 0.0, "zero")
+    mset(T.kt[:, 0:64], 0.0, "kt")
+    mset(T.bx[:], 0.0, "bx")
+    mset(T.xt[:], 0.0, "xt")
+    mset(T.maskb[:], BIG, "maskb")
+    mset(T.maskb[:, 0:16:5], 0.5, "maskb")
+    mset(T.cc[:, C:200], 4096.0, "ccx")
+    mset(T.kt[64:65, 2:64:4], -256.0, "kt")
+    mset(T.kt[64:65, 3:64:4], 1.0, "kt")
+    mset(T.kt[96:97, 2:64:4], 1.0, "kt")
+    mset(T.xt[64:65, 2:16:4], 1.0, "xt")
+    mset(T.xt[64:65, 18:32:4], -0.25, "xt")
+    mset(T.xt[64:65, 19:32:4], -8.0, "xt")
+    mset(T.xt[96:97, 18:32:4], -0.5, "xt")
+    for k in ("xq_in", "xhi", "xlo"):
+        res[k] = {"w": res["xt"]["w"], "r": []}
+
+    quant(T.p0[:, 0:128], T.q0[:, 0:128], T.tp[:], ["tp", "tpz"], ["p0", "q0"])
+    send(0)
+    iota(T.i1[:], [[1, 128]], 0, -1, "i1")
+    iota(T.vals[:], [[1, P]], C, 0, "vals")
+    iota(T.i8[:], [[1, C]], 0, -1, "i8", False)
+    iota(T.win1[:], [[1, 256]], -64, 0, "win1")
+
+    quant(T.w1[:, 64:256], T.v1[:, 64:256], T.tx[:], ["tx"], ["wb1", "vb1"])
+    for t in range(4):
+        ts(T.ur[:, t:512:4], T.ones[:], T.tu[:, t:t + 1], None, A.mult, None, ["ones", "tu"], ["ur%d" % t])
+    quant(T.urq[:], T.urs[:], T.ur[:], ["ur0", "ur1", "ur2", "ur3"], ["urq"])
+    ts(T.k1[:], T.i2[:], 0.0, -512.0, A.is_gt, A.mult, ["i2"], ["k1"])
+    ts(T.k2[:], T.i2[:], 0.0, 8192.0, A.is_equal, A.mult, ["i2"], ["k2"])
+    ts(T.i3b[:], T.i3[:], 15, None, A.bitwise_and, None, ["i3"], ["i3b"])
+    tt(T.kt[0:64, 0:64], T.k1[:], T.k2[:], A.add, ["k1", "k2"], ["kt"])
+    for t in range(2):
+        ts(T.kt[64:128, t:64:4], T.i3b[64:128, :], 0, 0.125, A.is_equal, A.mult, ["i3b"], ["kt"])
+    for k in (64, 128, 256):
+        op("V", lambda: V.tensor_copy(T.kt[:, k:2 * k], T.kt[:, 0:k]), ["kt"], ["kt"])
+    quant(T.kq[:], T.ks[:], T.kt[:], ["kt"], ["kq"])
+    for k in (0, 32):
+        ts(T.tri[k:k + 32, :], T.i4[:], 0.0, None, A.is_gt, None, ["i4"], ["tri%d" % k])
+    ts(T.m4a[:], T.i5[:], 0.0, None, A.is_ge, None, ["i5"], ["m4a"])
+    ts(T.m4b[:], T.i5[:], 16.0, None, A.is_lt, None, ["i5"], ["m4b"])
+    ts(T.i6b[:], T.i6[:], 15, None, A.bitwise_and, None, ["i6"], ["i6b"])
+    tt(T.mask4[:], T.m4a[:], T.m4b[:], A.mult, ["m4a", "m4b"], ["mask4"])
+    tt(T.islot[:], T.i6b[:], T.i7[:], A.add, ["i6b", "i7"], ["islot"])
+    ts(T.dcol[:], T.i6b[:, 0:1], 14.5, 1000.0, A.is_lt, A.mult, ["i6b"], ["dcol"])
+    mset(T.z0[:], 0.0, "z0")
+    mset(T.wide1[:], 0.0, "wide1")
+    mset(T.wide2[:], 0.0, "wide2")
+    ts(T.wide1[:, 3:515:4], T.i1[:], 0.0, None, A.is_equal, None, ["i1"], ["wide1"])
+    ts(T.wide2[:, 3:515:4], T.i1[:], 0.0, -0.5, A.is_equal, A.mult, ["i1"], ["wide2"])
+    for b in range(4):
+        quant(T["eq%d" % b][:], T["es%d" % b][:], T.wide1[:, 3 - b:515 - b], ["wide1"], ["eq%d" % b])
+    quant(T.p1[:, 64:192], T.q1[:, 64:192], T.z0[:], ["z0"], ["pz1"])
+    mset(T.zt[:, 256:512], 0.0, "ztz")
+    for b in range(4):
+        quant(T["nq%d" % b][:], T["ns%d" % b][:], T.wide2[:, 3 - b:515 - b], ["wide2"], ["nq%d" % b])
+    ts(T.i8b[:], T.i8[:], 15, None, A.bitwise_and, None, ["i8"], ["i8b"])
+    ts(T.s1[:], T.i8b[:], 0, -4000.0, A.is_equal, A.mult, ["i8b"], ["s1"])
+    ts(T.s2[:], T.i8b[:], 1, 1000.0, A.is_equal, A.mult, ["i8b"], ["s2"])
+    tt(T.seg[:], T.s1[:], T.s2[:], A.add, ["s1", "s2"], ["seg"])
+    quant(T.wq[:], T.ws[:], T.tw[:], ["tw"], ["wq"])
+    for h in range(2, H + 1):
+        act(T["win%d" % h][:], T.win1[:], F.Copy, ["win1"], ["win%d" % h])
+
+    def urow(h):
+        mm(T.pur[:, 0:C], T.urq[:], T.urs[:], T["w%d" % h][:, 64:256], T["v%d" % h][:, 64:256], ["urq", "wb%d" % h, "vb%d" % h], ["pur"])
+
+    urow(1)
+    for h in range(1, H + 1):
+        w, v, p, q = T["w%d" % h], T["v%d" % h], T["p%d" % h], T["q%d" % h]
+        w2, v2 = T["w%d" % (h + 1)], T["v%d" % (h + 1)]
+        off, tof, win = T["off%d" % h], T["tof%d" % h], T["win%d" % h]
+        got = 2 * len(lanes(prv, core))
+        last["arr%d" % h] = got
+        wa, wb, vb = "wa%d" % h, "wb%d" % h, "vb%d" % h
+        res[wa] = {"w": ("arr%d" % h, got, {}), "r": []}
+        pan = [wa, wb, vb]
+        mm(T.puc[:, 0:128], w[:, 0:128], v[:, 0:128], T.urq[:], T.urs[:], pan + ["urq"], ["puc"])
+        mm(T.psc_[:, 0:C], w[:, 0:128], v[:, 0:128], w[:, 64:256], v[:, 64:256], pan, ["psc_"])
+        for b in range(4):
+            mm(T["pd%d" % b][:, 0:128], T["eq%d" % b][:], T["es%d" % b][:], w[:, 0:128], v[:, 0:128], pan + ["eq%d" % b], ["pd%d" % b], True, False)
+        act(T.ucol[:], T.puc[0:64, 0:1], F.Copy, ["puc"], ["ucol"])
+        act(T.sgn[:], T.pur[0:64, 0:C], F.Sign, ["pur", "ucol"], ["sgn"], bias=T.ucol[:], scale=-1.0)
+        op("V", lambda: V.tensor_tensor_scan(T.rr[:], T.psc_[0:64, 0:C], T.zero[:], -1.0e29, A.max, A.add), ["psc_", "zero"], ["rr"])
+        ts(T.lt[:], T.rr[:], T.rr[:, C - 1:C], 2048.0, A.is_lt, A.mult, ["rr"], ["lt"])
+        tt(T.cc[:, 0:C], T.sgn[:], T.idx[:], A.add, ["sgn", "idx"], ["cc"])
+        op("V", lambda: V.tensor_tensor_scan(T.vs[:], T.lt[:], T.cc[:, 1:C + 1], T.cc[:, 0:1], A.max, A.min), ["lt", "cc", "ccx"], ["vs"])
+        val = T.vs[:, C - 1:C]
+        ts(T.tc[:], val, M4, M4, A.add, A.subtract, ["vs"], ["tc"])
+        ts(T.bx[:, 32:64], T.tri[:], T.tc[:], None, A.mult, None, ["tri0", "tri32", "tc"], ["bx"])
+        ts(T.bx[32:64, 0:32], T.ones[0:32, 0:32], T.tc[0:32, :], None, A.mult, None, ["ones", "tc"], ["bx2"])
+        op("V", lambda: V.transpose(T.by[:], T.bx[:]), ["bx", "bx2"], ["by"])
+        ts(T.mm[64:128, :], T.mask4[:], T.tc[:], None, A.mult, None, ["mask4", "tc"], ["mm"])
+        ts(T.hb[:], T.tc[:], val, BIG, A.is_le, A.mult, ["tc", "vs"], ["hb"])
+        ts(T.xt[64:128, 16:32:4], T.mm[64:128, :], M128, M128, A.add, A.subtract, ["mm"], ["xhi"])
+        ts(T.ne[:], T.by[:], T.tc[:], None, A.not_equal, None, ["by", "tc"], ["ne"])
+        tt(T.xt[64:128, 17:32:4], T.mm[64:128, :], T.xt[64:128, 16:32:4], A.subtract, ["mm", "xhi"], ["xlo"])
+        op("V", lambda: V.tensor_reduce(T.own[:], T.ne[:], AxisListType.X, A.min), ["ne"], ["own"])
+        ts(T.xt[0:64, 0:16], T.maskb[:], T.hb[:], T.own[:], A.max, A.is_lt, ["maskb", "hb", "own"], ["xq_in"])
+        quant(T.xq[:], T.xs[:], T.xt[:], ["xt", "xq_in", "xhi", "xlo"], ["xq"])
+        mm(T.pk[:, 0:128], T.kq[:], T.ks[:], T.xq[:], T.xs[:], ["kq", "xq"], ["pk"])
+        for c in range(4):
+            ts(off[:, c:c + 1], T.pk[:, c:c + 1], T.pk[:, 4 + c:5 + c], T.islot[:, c:c + 1], A.min, A.max, ["pk", "islot"], ["off%d_%d" % (h, c)])
+        offs = ["off%d_%d" % (h, c) for c in range(4)]
+        op("V", lambda: V.tensor_copy(p[:, 0:P].bitcast(dt.uint32), w[:, 0:256].bitcast(dt.uint32).indirect(off[:, 0:4])), offs + pan, ["p%d" % h])
+        act(q[:, 0:P], v[:, 0:256].indirect(off[:, 0:4]), F.Copy, offs + pan, ["q%d" % h])
+        if h < H:
+            send(h)
+        pq = ["p%d" % h, "q%d" % h, "pz%d" % h]
+        for b in (0, 2, 1, 3):
+            mm(T["pd%d" % b][:, 0:128], T["nq%d" % b][:], T["ns%d" % b][:], p[:, 0:128], q[:, 0:128], pq + ["nq%d" % b], ["pd%d" % b], False, True)
+        mm(T.puc[:, 0:128], T.wq[:], T.ws[:], p[:, 0:128], q[:, 0:128], pq + ["wq"], ["puc"])
+        op("V", lambda: V.tensor_copy(win[:].indirect(off[:, 0:4]), T.vals[:]), offs + ["vals", "win%d" % h], ["win%d" % h])
+        op("V", lambda: V.tensor_tensor_scan(T.scn[:], T.seg[:], win[:, 64:256], 0.0, A.add, A.max), ["seg", "win%d" % h], ["scn"])
+        for b in (0, 1):
+            op("V", lambda: V.tensor_copy(T.zt[:, b:256:4], T["pd%d" % b][:, 0:P]), ["pd%d" % b], ["zt%d" % b])
+        for b in (2, 3):
+            act(T.zt[:, b:256:4], T["pd%d" % b][:, 0:P], F.Copy, ["pd%d" % b], ["zt%d" % b])
+        ts(tof[:], T.scn[:, 15:C:16], T.dcol[:], None, A.subtract, None, ["scn", "dcol"], ["tof%d" % h])
+        quant(w[:, 256:384], v[:, 256:384], T.zt[:], ["zt0", "zt1", "zt2", "zt3", "ztz"], ["wz%d" % h])
+        act(T.ys[:, (h - 1) * P:h * P], T.puc[:, 0:P], F.Copy, ["puc"], ["ys%d" % h])
+        tab = [wb, vb, "wz%d" % h, "tof%d" % h]
+        op("V", lambda: V.tensor_copy(w2[:, 64:256].bitcast(dt.uint32), w[:, 64:384].bitcast(dt.uint32).indirect(tof[:, 0:12])), tab, ["wb%d" % (h + 1)])
+        act(v2[:, 64:256], v[:, 64:384].indirect(tof[:, 0:12]), F.Copy, tab, ["vb%d" % (h + 1)])
+        if h < H:
+            urow(h + 1)
+        if h == 1:
+            for k in range(2, H + 1):
+                quant(T["p%d" % k][:, 64:192], T["q%d" % k][:, 64:192], T.z0[:], ["z0"], ["pz%d" % k])
+        if h == H:
+            dma("Y", T.pc[:], p[:, 0:P].bitcast(dt.uint8), "fin", ["p%d" % h], [])
+            for k in range(4):
+                dma("Y", T.psc[4 * k:4 * k + 4, :], q[32 * k:32 * k + 4, 0:P], "fin", ["q%d" % h], [])
+        dma("Y", T.y[:, (h - 1) * P:h * P], T.ys[:, (h - 1) * P:h * P], "st%d" % h, ["ys%d" % h], [])
+    e = H + 1
+    dma("Y", T.oc[:], T["w%d" % e][:, 64:256].bitcast(dt.uint8), "fin", ["wb%d" % e], [])
+    for k in range(4):
+        dma("S" if k % 2 else "Y", T.osc[4 * k:4 * k + 4, :], T["v%d" % e][32 * k:32 * k + 4, 64:256], "fin", ["vb%d" % e], [])
+    for sem in sorted(last):
+        need("G", (sem, last[sem], {}))

@@ -15,31 +15,31 @@ def _sb(dtype, **shapes):
         SCRATCH[name] = ("sbuf", list(shapes[name]), dtype)
 
 
-_sb(BF16, tp=(128, 512), tx=(128, 768), tw=(128, 512), tu=(128, 4), ur=(128, 512), z0=(128, 512), wide1=(128, 516), wide2=(128, 516),
-    kt=(128, 512), xt=(128, 512), zt=(128, 512), vals=(128, P), sgn=(64, C), lt=(64, C), ne=(64, 64))
-_sb(F32, ones=(128, 128), zero=(64, C), i1=(128, 128), i2=(64, 64), k1=(64, 64), k2=(64, 64), i4=(32, 32), tri=(64, 32), i5=(64, 4),
-    m4a=(64, 4), m4b=(64, 4), mask4=(64, 4), islot=(128, 4), dcol=(128, 1), s1=(128, C), s2=(128, C), seg=(128, C), idx=(64, C),
-    maskb=(64, 16), ucol=(64, 1), cc=(64, 200), rr=(64, C), vs=(64, C), tc=(64, 1), hb=(64, 1), own=(64, 1), bx=(64, 64), by=(64, 64),
-    mm=(128, 4), scn=(128, C), ys=(128, H * P))
-_sb(I32, i3=(128, 16), i3b=(128, 16), i6=(128, 4), i6b=(128, 4), i7=(128, 4), i8=(128, C), i8b=(128, C))
-_sb(F8, urq=(128, 128), wq=(128, 128), kq=(128, 128), xq=(128, 128))
-_sb(U8, urs=(128, 128), ws=(128, 128), ks=(128, 128), xs=(128, 128))
+_sb(BF16, tp=(128, 512), tx=(128, 768), tw=(128, 512), tu=(128, 4), ur=(128, 768), nur=(128, 512), wide1=(128, 516), wide2=(128, 516),
+    kt=(128, 512), xt=(128, 512), zt=(128, 512), vals=(128, P), sgn=(64, C), lt=(64, C))
+_sb(F32, ones=(32, 32), zero=(128, C), i1=(128, 128), i2=(64, 64), k1=(64, 64), k2=(64, 64), i4=(32, 32), tri=(64, 32), i5=(64, 4),
+    m4a=(64, 4), m4b=(64, 4), mask4=(64, 4), islot=(128, 4), dcol=(128, 1), s1=(128, 16), s2=(128, 16), seg=(128, C), idx=(64, C),
+    maskb=(64, 16), cc=(64, 200), rr=(64, C), vs=(64, C), tc=(64, 1), hb=(64, 1), own=(64, 1), bx=(64, 64), by=(64, 64),
+    ne=(64, 64), mm=(128, 4), scn=(128, C), ys=(128, H * P))
+_sb(I32, i3=(128, 16), i3b=(128, 16), i6=(128, 4), i6b=(128, 4), i7=(128, 4))
+_sb(F8, urq=(128, C), nuq=(128, 128), wq=(128, 128), kq=(128, 128), xq=(128, 128))
+_sb(U8, urs=(128, C), nus=(128, 128), ws=(128, 128), ks=(128, 128), xs=(128, 128))
 for _h in range(1, H + 2):
     _sb(F8, **{"w%d" % _h: (128, 384)})
     _sb(U8, **{"v%d" % _h: (128, 384)})
 for _h in range(H + 1):
-    _sb(F8, **{"p%d" % _h: (128, 192)})
-    _sb(U8, **{"q%d" % _h: (128, 192)})
+    _sb(F8, **{"p%d" % _h: (128, 128)})
+    _sb(U8, **{"q%d" % _h: (128, 128)})
 for _h in range(1, H + 1):
     _sb(U16, **{"off%d" % _h: (128, 4), "tof%d" % _h: (128, 12)})
     _sb(BF16, **{"win%d" % _h: (128, 256)})
 for _b in range(4):
     _sb(F8, **{"eq%d" % _b: (128, 128), "nq%d" % _b: (128, 128)})
     _sb(U8, **{"es%d" % _b: (128, 128), "ns%d" % _b: (128, 128)})
-for _n in ("psc_", "pur", "puc", "pk", "pd0", "pd1", "pd2", "pd3"):
+for _n in ("psc_", "pur", "py", "pk", "pd0", "pd1", "pd2", "pd3"):
     SCRATCH[_n] = ("psum", [128, 512], F32)
 
-SEMAPHORES = ["cV", "cP", "cS", "cG", "lp", "lx", "lu", "lw", "fin"]
+SEMAPHORES = ["cV", "cP", "cS", "cG", "lp", "lx", "lu", "lw", "pad", "fin"]
 SEMAPHORES += ["arr%d" % h for h in range(1, H + 1)] + ["snt%d" % h for h in range(H)] + ["st%d" % h for h in range(1, H + 1)]
 
 
@@ -115,6 +115,9 @@ def rank_program(g, core, T, topo):
     def tt(out, a, b, o, reads, writes):
         op("V", lambda: V.tensor_tensor(out, a, b, o), reads, writes)
 
+    def scan(out, a, b, init, o0, o1, reads, writes):
+        op("V", lambda: V.tensor_tensor_scan(out, a, b, init, o0, o1), reads, writes)
+
     def quant(q, s, t, reads, writes):
         op("V", lambda: V.quantize_mx(q, s, t), reads, writes)
 
@@ -154,47 +157,47 @@ def rank_program(g, core, T, topo):
     iota(T.i5[:], [[-16, 4]], 0, 1, "i5")
     iota(T.i6[:], [[0, 4]], 0, 1, "i6", False)
     iota(T.i7[:], [[16, 4]], 0, 0, "i7", False)
-    iota(T.idx[:], [[8, C]], 68, 0, "idx")
 
     mset(T.tp[:, 256:512], 0.0, "tpz")
-    mset(T.ones[:], 1.0, "ones")
     mset(T.zero[:], 0.0, "zero")
     mset(T.kt[:, 0:64], 0.0, "kt")
-    mset(T.bx[:], 0.0, "bx")
     mset(T.xt[:], 0.0, "xt")
     mset(T.maskb[:], BIG, "maskb")
-    mset(T.maskb[:, 0:16:5], 0.5, "maskb")
+    mset(T.bx[:], 0.0, "bx")
     mset(T.cc[:, C:200], 4096.0, "ccx")
-    mset(T.kt[64:65, 2:64:4], -256.0, "kt")
-    mset(T.kt[64:65, 3:64:4], 1.0, "kt")
-    mset(T.kt[96:97, 2:64:4], 1.0, "kt")
-    mset(T.xt[64:65, 2:16:4], 1.0, "xt")
-    mset(T.xt[64:65, 18:32:4], -0.25, "xt")
-    mset(T.xt[64:65, 19:32:4], -8.0, "xt")
-    mset(T.xt[96:97, 18:32:4], -0.5, "xt")
-    for k in ("xq_in", "xhi", "xlo"):
-        res[k] = {"w": res["xt"]["w"], "r": []}
+    mset(T.ones[:], 1.0, "ones")
+    mset(T.wide1[:], 0.0, "wide1")
+    mset(T.maskb[:, 0:16:5], 4.0, "maskb")
+    for (t, part, col, val) in ((T.kt, 64, 2, -256.0), (T.kt, 64, 3, 1.0), (T.kt, 96, 2, 1.0)):
+        op("V", lambda: V.memset(t[part:part + 1, col:64:4], val), ["kt"], ["kt%d%d" % (part, col)])
+    for (part, a, b, val) in ((64, 2, 16, 1.0), (64, 18, 32, -0.25), (64, 19, 32, -8.0), (96, 18, 32, -0.5)):
+        op("V", lambda: V.memset(T.xt[part:part + 1, a:b:4], val), ["xt"], ["xt%d%d" % (part, a)])
+    xcon = ["xt", "xt642", "xt6418", "xt6419", "xt9618"]
+    kcon = ["kt", "kt642", "kt643", "kt962"]
 
-    quant(T.p0[:, 0:128], T.q0[:, 0:128], T.tp[:], ["tp", "tpz"], ["p0", "q0"])
+    quant(T.p0[:], T.q0[:], T.tp[:], ["tp", "tpz"], ["p0", "q0"])
     send(0)
     iota(T.i1[:], [[1, 128]], 0, -1, "i1")
+    iota(T.idx[:], [[8, C]], 68, 0, "idx")
     iota(T.vals[:], [[1, P]], C, 0, "vals")
-    iota(T.i8[:], [[1, C]], 0, -1, "i8", False)
     iota(T.win1[:], [[1, 256]], -64, 0, "win1")
 
-    quant(T.w1[:, 64:256], T.v1[:, 64:256], T.tx[:], ["tx"], ["wb1", "vb1"])
     for t in range(4):
-        ts(T.ur[:, t:512:4], T.ones[:], T.tu[:, t:t + 1], None, A.mult, None, ["ones", "tu"], ["ur%d" % t])
-    quant(T.urq[:], T.urs[:], T.ur[:], ["ur0", "ur1", "ur2", "ur3"], ["urq"])
+        act(T.ur[:, t:768:4], T.zero[:], F.Identity, ["zero", "tu"], ["ur%d" % t], bias=T.tu[:, t:t + 1])
+    act(T.nur[:], T.ur[:, 0:512], F.Copy, ["ur0", "ur1", "ur2", "ur3"], ["nur"], scale=-1.0)
+    quant(T.w1[:, 64:256], T.v1[:, 64:256], T.tx[:], ["tx"], ["wb1", "vb1"])
     ts(T.k1[:], T.i2[:], 0.0, -512.0, A.is_gt, A.mult, ["i2"], ["k1"])
     ts(T.k2[:], T.i2[:], 0.0, 8192.0, A.is_equal, A.mult, ["i2"], ["k2"])
     ts(T.i3b[:], T.i3[:], 15, None, A.bitwise_and, None, ["i3"], ["i3b"])
-    tt(T.kt[0:64, 0:64], T.k1[:], T.k2[:], A.add, ["k1", "k2"], ["kt"])
+    tt(T.kt[0:64, 0:64], T.k1[:], T.k2[:], A.add, ["k1", "k2", "kt"], ["ktl"])
     for t in range(2):
-        ts(T.kt[64:128, t:64:4], T.i3b[64:128, :], 0, 0.125, A.is_equal, A.mult, ["i3b"], ["kt"])
+        ts(T.kt[64:128, t:64:4], T.i3b[64:128, :], 0, 0.125, A.is_equal, A.mult, ["i3b", "kt"], ["kth%d" % t])
+    kcon += ["ktl", "kth0", "kth1"]
     for k in (64, 128, 256):
-        op("V", lambda: V.tensor_copy(T.kt[:, k:2 * k], T.kt[:, 0:k]), ["kt"], ["kt"])
-    quant(T.kq[:], T.ks[:], T.kt[:], ["kt"], ["kq"])
+        act(T.kt[:, k:2 * k], T.kt[:, 0:k], F.Copy, list(kcon), ["ktc%d" % k])
+        kcon.append("ktc%d" % k)
+    ts(T.wide1[:, 3:515:4], T.i1[:], 0.0, None, A.is_equal, None, ["i1"], ["wide1"])
+    act(T.wide2[:], T.wide1[:], F.Copy, ["wide1"], ["wide2"], scale=-0.5)
     for k in (0, 32):
         ts(T.tri[k:k + 32, :], T.i4[:], 0.0, None, A.is_gt, None, ["i4"], ["tri%d" % k])
     ts(T.m4a[:], T.i5[:], 0.0, None, A.is_ge, None, ["i5"], ["m4a"])
@@ -202,28 +205,15 @@ def rank_program(g, core, T, topo):
     ts(T.i6b[:], T.i6[:], 15, None, A.bitwise_and, None, ["i6"], ["i6b"])
     tt(T.mask4[:], T.m4a[:], T.m4b[:], A.mult, ["m4a", "m4b"], ["mask4"])
     tt(T.islot[:], T.i6b[:], T.i7[:], A.add, ["i6b", "i7"], ["islot"])
-    ts(T.dcol[:], T.i6b[:, 0:1], 14.5, 1000.0, A.is_lt, A.mult, ["i6b"], ["dcol"])
-    mset(T.z0[:], 0.0, "z0")
-    mset(T.wide1[:], 0.0, "wide1")
-    mset(T.wide2[:], 0.0, "wide2")
-    ts(T.wide1[:, 3:515:4], T.i1[:], 0.0, None, A.is_equal, None, ["i1"], ["wide1"])
-    ts(T.wide2[:, 3:515:4], T.i1[:], 0.0, -0.5, A.is_equal, A.mult, ["i1"], ["wide2"])
+    quant(T.nuq[:], T.nus[:], T.nur[:], ["nur"], ["nuq"])
+    quant(T.urq[:], T.urs[:], T.ur[:], ["ur0", "ur1", "ur2", "ur3"], ["urq"])
+    quant(T.kq[:], T.ks[:], T.kt[:], kcon, ["kq"])
     for b in range(4):
         quant(T["eq%d" % b][:], T["es%d" % b][:], T.wide1[:, 3 - b:515 - b], ["wide1"], ["eq%d" % b])
-    quant(T.p1[:, 64:192], T.q1[:, 64:192], T.z0[:], ["z0"], ["pz1"])
     mset(T.zt[:, 256:512], 0.0, "ztz")
-    for b in range(4):
-        quant(T["nq%d" % b][:], T["ns%d" % b][:], T.wide2[:, 3 - b:515 - b], ["wide2"], ["nq%d" % b])
-    ts(T.i8b[:], T.i8[:], 15, None, A.bitwise_and, None, ["i8"], ["i8b"])
-    ts(T.s1[:], T.i8b[:], 0, -4000.0, A.is_equal, A.mult, ["i8b"], ["s1"])
-    ts(T.s2[:], T.i8b[:], 1, 1000.0, A.is_equal, A.mult, ["i8b"], ["s2"])
-    tt(T.seg[:], T.s1[:], T.s2[:], A.add, ["s1", "s2"], ["seg"])
-    quant(T.wq[:], T.ws[:], T.tw[:], ["tw"], ["wq"])
-    for h in range(2, H + 1):
-        act(T["win%d" % h][:], T.win1[:], F.Copy, ["win1"], ["win%d" % h])
 
     def urow(h):
-        mm(T.pur[:, 0:C], T.urq[:], T.urs[:], T["w%d" % h][:, 64:256], T["v%d" % h][:, 64:256], ["urq", "wb%d" % h, "vb%d" % h], ["pur"])
+        mm(T.pur[:, 0:C], T.nuq[:], T.nus[:], T["w%d" % h][:, 64:256], T["v%d" % h][:, 64:256], ["nuq", "wb%d" % h, "vb%d" % h], ["pur"], True, False)
 
     urow(1)
     for h in range(1, H + 1):
@@ -235,29 +225,35 @@ def rank_program(g, core, T, topo):
         wa, wb, vb = "wa%d" % h, "wb%d" % h, "vb%d" % h
         res[wa] = {"w": ("arr%d" % h, got, {}), "r": []}
         pan = [wa, wb, vb]
-        mm(T.puc[:, 0:128], w[:, 0:128], v[:, 0:128], T.urq[:], T.urs[:], pan + ["urq"], ["puc"])
         mm(T.psc_[:, 0:C], w[:, 0:128], v[:, 0:128], w[:, 64:256], v[:, 64:256], pan, ["psc_"])
+        mm(T.pur[:, 0:C], w[:, 0:128], v[:, 0:128], T.urq[:], T.urs[:], pan + ["urq"], ["pur"], False, True)
         for b in range(4):
             mm(T["pd%d" % b][:, 0:128], T["eq%d" % b][:], T["es%d" % b][:], w[:, 0:128], v[:, 0:128], pan + ["eq%d" % b], ["pd%d" % b], True, False)
-        act(T.ucol[:], T.puc[0:64, 0:1], F.Copy, ["puc"], ["ucol"])
-        act(T.sgn[:], T.pur[0:64, 0:C], F.Sign, ["pur", "ucol"], ["sgn"], bias=T.ucol[:], scale=-1.0)
-        op("V", lambda: V.tensor_tensor_scan(T.rr[:], T.psc_[0:64, 0:C], T.zero[:], -1.0e29, A.max, A.add), ["psc_", "zero"], ["rr"])
+        act(T.sgn[:], T.pur[0:64, 0:C], F.Sign, ["pur"], ["sgn"])
+        if h == 1:
+            for k in range(1, H + 1):
+                for (d, s, c) in ((T["p%d" % k][:, P:128].bitcast(dt.uint8), T.p0[:, P:128].bitcast(dt.uint8), "pz%d"), (T["q%d" % k][:, P:128], T.q0[:, P:128], "qz%d")):
+                    dma("Y", d, s, "pad", ["p0", wa], [c % k])
+            for k in range(1, H + 1):
+                for c in ("pz%d", "qz%d"):
+                    res[c % k] = {"w": ("pad", last["pad"], {}), "r": []}
+        scan(T.rr[:], T.psc_[0:64, 0:C], T.zero[0:64, :], -1.0e29, A.max, A.add, ["psc_", "zero"], ["rr"])
         ts(T.lt[:], T.rr[:], T.rr[:, C - 1:C], 2048.0, A.is_lt, A.mult, ["rr"], ["lt"])
-        tt(T.cc[:, 0:C], T.sgn[:], T.idx[:], A.add, ["sgn", "idx"], ["cc"])
-        op("V", lambda: V.tensor_tensor_scan(T.vs[:], T.lt[:], T.cc[:, 1:C + 1], T.cc[:, 0:1], A.max, A.min), ["lt", "cc", "ccx"], ["vs"])
+        scan(T.cc[:, 0:C], T.idx[:], T.sgn[:], 0.0, A.max, A.add, ["sgn", "idx"], ["cc"])
+        scan(T.vs[:], T.lt[:], T.cc[:, 1:C + 1], T.cc[:, 0:1], A.max, A.min, ["lt", "cc", "ccx"], ["vs"])
         val = T.vs[:, C - 1:C]
+        ts(T.bx[:, 32:64], T.tri[:], val, None, A.mult, None, ["tri0", "tri32", "vs"], ["bx"])
+        ts(T.bx[32:64, 0:32], T.ones[:], val[0:32, :] if False else T.vs[0:32, C - 1:C], None, A.mult, None, ["ones", "vs"], ["bx2"])
         ts(T.tc[:], val, M4, M4, A.add, A.subtract, ["vs"], ["tc"])
-        ts(T.bx[:, 32:64], T.tri[:], T.tc[:], None, A.mult, None, ["tri0", "tri32", "tc"], ["bx"])
-        ts(T.bx[32:64, 0:32], T.ones[0:32, 0:32], T.tc[0:32, :], None, A.mult, None, ["ones", "tc"], ["bx2"])
         op("V", lambda: V.transpose(T.by[:], T.bx[:]), ["bx", "bx2"], ["by"])
         ts(T.mm[64:128, :], T.mask4[:], T.tc[:], None, A.mult, None, ["mask4", "tc"], ["mm"])
+        ts(T.ne[:], T.by[:], val, None, A.subtract, None, ["by", "vs"], ["ne"])
         ts(T.hb[:], T.tc[:], val, BIG, A.is_le, A.mult, ["tc", "vs"], ["hb"])
-        ts(T.xt[64:128, 16:32:4], T.mm[64:128, :], M128, M128, A.add, A.subtract, ["mm"], ["xhi"])
-        ts(T.ne[:], T.by[:], T.tc[:], None, A.not_equal, None, ["by", "tc"], ["ne"])
+        ts(T.xt[64:128, 16:32:4], T.mm[64:128, :], M128, M128, A.add, A.subtract, ["mm", "xt"], ["xhi"])
+        op("V", lambda: V.tensor_reduce(T.own[:], T.ne[:], AxisListType.X, A.min, apply_absolute_value=True), ["ne"], ["own"])
         tt(T.xt[64:128, 17:32:4], T.mm[64:128, :], T.xt[64:128, 16:32:4], A.subtract, ["mm", "xhi"], ["xlo"])
-        op("V", lambda: V.tensor_reduce(T.own[:], T.ne[:], AxisListType.X, A.min), ["ne"], ["own"])
-        ts(T.xt[0:64, 0:16], T.maskb[:], T.hb[:], T.own[:], A.max, A.is_lt, ["maskb", "hb", "own"], ["xq_in"])
-        quant(T.xq[:], T.xs[:], T.xt[:], ["xt", "xq_in", "xhi", "xlo"], ["xq"])
+        ts(T.xt[0:64, 0:16], T.maskb[:], T.hb[:], T.own[:], A.max, A.is_lt, ["maskb", "hb", "own", "xt"], ["xq_in"])
+        quant(T.xq[:], T.xs[:], T.xt[:], xcon + ["xq_in", "xhi", "xlo"], ["xq"])
         mm(T.pk[:, 0:128], T.kq[:], T.ks[:], T.xq[:], T.xs[:], ["kq", "xq"], ["pk"])
         for c in range(4):
             ts(off[:, c:c + 1], T.pk[:, c:c + 1], T.pk[:, 4 + c:5 + c], T.islot[:, c:c + 1], A.min, A.max, ["pk", "islot"], ["off%d_%d" % (h, c)])
@@ -266,19 +262,29 @@ def rank_program(g, core, T, topo):
         act(q[:, 0:P], v[:, 0:256].indirect(off[:, 0:4]), F.Copy, offs + pan, ["q%d" % h])
         if h < H:
             send(h)
-        pq = ["p%d" % h, "q%d" % h, "pz%d" % h]
+        if h == 1:
+            for b in range(4):
+                quant(T["nq%d" % b][:], T["ns%d" % b][:], T.wide2[:, 3 - b:515 - b], ["wide2"], ["nq%d" % b])
+            quant(T.wq[:], T.ws[:], T.tw[:], ["tw"], ["wq"])
+            ts(T.s1[:], T.i3b[:], 0, -4000.0, A.is_equal, A.mult, ["i3b"], ["s1"])
+            ts(T.s2[:], T.i3b[:], 1, 1000.0, A.is_equal, A.mult, ["i3b"], ["s2"])
+            ts(T.dcol[:], T.i6b[:, 0:1], 14.5, 1000.0, A.is_lt, A.mult, ["i6b"], ["dcol"])
+            tt(T.seg[:, 0:16], T.s1[:], T.s2[:], A.add, ["s1", "s2"], ["seg"])
+            for (a, b) in ((16, 32), (32, 64), (64, 128), (128, 192)):
+                act(T.seg[:, a:b], T.seg[:, 0:b - a], F.Copy, ["seg"], ["seg"])
+        pq = ["p%d" % h, "q%d" % h, "pz%d" % h, "qz%d" % h]
         for b in (0, 2, 1, 3):
-            mm(T["pd%d" % b][:, 0:128], T["nq%d" % b][:], T["ns%d" % b][:], p[:, 0:128], q[:, 0:128], pq + ["nq%d" % b], ["pd%d" % b], False, True)
-        mm(T.puc[:, 0:128], T.wq[:], T.ws[:], p[:, 0:128], q[:, 0:128], pq + ["wq"], ["puc"])
+            mm(T["pd%d" % b][:, 0:128], T["nq%d" % b][:], T["ns%d" % b][:], p[:], q[:], pq + ["nq%d" % b], ["pd%d" % b], False, True)
+        mm(T.py[:, 0:128], T.wq[:], T.ws[:], p[:], q[:], pq + ["wq"], ["py"])
         op("V", lambda: V.tensor_copy(win[:].indirect(off[:, 0:4]), T.vals[:]), offs + ["vals", "win%d" % h], ["win%d" % h])
-        op("V", lambda: V.tensor_tensor_scan(T.scn[:], T.seg[:], win[:, 64:256], 0.0, A.add, A.max), ["seg", "win%d" % h], ["scn"])
+        scan(T.scn[:], T.seg[:], win[:, 64:256], 0.0, A.add, A.max, ["seg", "win%d" % h], ["scn"])
         for b in (0, 1):
             op("V", lambda: V.tensor_copy(T.zt[:, b:256:4], T["pd%d" % b][:, 0:P]), ["pd%d" % b], ["zt%d" % b])
         for b in (2, 3):
             act(T.zt[:, b:256:4], T["pd%d" % b][:, 0:P], F.Copy, ["pd%d" % b], ["zt%d" % b])
         ts(tof[:], T.scn[:, 15:C:16], T.dcol[:], None, A.subtract, None, ["scn", "dcol"], ["tof%d" % h])
         quant(w[:, 256:384], v[:, 256:384], T.zt[:], ["zt0", "zt1", "zt2", "zt3", "ztz"], ["wz%d" % h])
-        act(T.ys[:, (h - 1) * P:h * P], T.puc[:, 0:P], F.Copy, ["puc"], ["ys%d" % h])
+        act(T.ys[:, (h - 1) * P:h * P], T.py[:, 0:P], F.Copy, ["py"], ["ys%d" % h])
         tab = [wb, vb, "wz%d" % h, "tof%d" % h]
         op("V", lambda: V.tensor_copy(w2[:, 64:256].bitcast(dt.uint32), w[:, 64:384].bitcast(dt.uint32).indirect(tof[:, 0:12])), tab, ["wb%d" % (h + 1)])
         act(v2[:, 64:256], v[:, 64:384].indirect(tof[:, 0:12]), F.Copy, tab, ["vb%d" % (h + 1)])
@@ -286,7 +292,7 @@ def rank_program(g, core, T, topo):
             urow(h + 1)
         if h == 1:
             for k in range(2, H + 1):
-                quant(T["p%d" % k][:, 64:192], T["q%d" % k][:, 64:192], T.z0[:], ["z0"], ["pz%d" % k])
+                iota(T["win%d" % k][:], [[1, 256]], -64, 0, "win%d" % k)
         if h == H:
             dma("Y", T.pc[:], p[:, 0:P].bitcast(dt.uint8), "fin", ["p%d" % h], [])
             for k in range(4):

@@ -3,7 +3,6 @@ from concourse.mybir import dt, AluOpType as A, AxisListType, ActivationFunction
 
 P, C, H = 64, 192, 4
 BIG = 1.0e6
-M4 = 1.5 * 2.0 ** 25
 M128 = 1.5 * 2.0 ** 30
 F32, BF16, I32, U16, F8, U8 = "float32", "bfloat16", "int32", "uint16", "float8_e4m3fn_x4", "uint8"
 
@@ -16,11 +15,11 @@ def _sb(dtype, **shapes):
 
 
 _sb(BF16, tp=(128, 512), tx=(128, 768), tw=(128, 512), tu=(128, 4), ur=(128, 768), nur=(128, 512), wide1=(128, 516), wide2=(128, 516),
-    kt=(128, 512), xt=(128, 512), zt=(128, 512), vals=(128, P), sgn=(64, C), lt=(64, C))
-_sb(F32, ones=(32, 32), zero=(128, C), i1=(128, 128), i2=(64, 64), k1=(64, 64), k2=(64, 64), i4=(32, 32), tri=(64, 32), i5=(64, 4),
+    kt=(128, 512), xt=(128, 512), zt=(128, 512), z0=(128, 512), vals=(128, P), sgn=(64, C), lt=(64, C), less=(64, C), ne=(64, 64))
+_sb(F32, zero=(128, C), i1=(128, 128), i2=(64, 64), k1=(64, 64), k2=(64, 64), i4=(32, 32), tri=(64, 32), i5=(64, 4),
     m4a=(64, 4), m4b=(64, 4), mask4=(64, 4), islot=(128, 4), dcol=(128, 1), s1=(128, 16), s2=(128, 16), seg=(128, C), idx=(64, C),
-    maskb=(64, 16), cc=(64, 200), rr=(64, C), vs=(64, C), tc=(64, 1), hb=(64, 1), own=(64, 1), bx=(64, 64), by=(64, 64),
-    ne=(64, 64), mm=(128, 4), scn=(128, C), ys=(128, H * P))
+    maskb=(64, 16), cc=(64, 200), rr=(64, C), vs=(64, C), pl=(64, 1), tc=(64, 1), hb=(64, 1), own=(64, 1), bx=(64, 64), by=(64, 64),
+    mm=(128, 4), scn=(128, C), ys=(128, H * P))
 _sb(I32, i3=(128, 16), i3b=(128, 16), i6=(128, 4), i6b=(128, 4), i7=(128, 4))
 _sb(F8, urq=(128, C), nuq=(128, 128), wq=(128, 128), kq=(128, 128), xq=(128, 128))
 _sb(U8, urs=(128, C), nus=(128, 128), ws=(128, 128), ks=(128, 128), xs=(128, 128))
@@ -28,8 +27,8 @@ for _h in range(1, H + 2):
     _sb(F8, **{"w%d" % _h: (128, 384)})
     _sb(U8, **{"v%d" % _h: (128, 384)})
 for _h in range(H + 1):
-    _sb(F8, **{"p%d" % _h: (128, 128)})
-    _sb(U8, **{"q%d" % _h: (128, 128)})
+    _sb(F8, **{"p%d" % _h: (128, 192)})
+    _sb(U8, **{"q%d" % _h: (128, 192)})
 for _h in range(1, H + 1):
     _sb(U16, **{"off%d" % _h: (128, 4), "tof%d" % _h: (128, 12)})
     _sb(BF16, **{"win%d" % _h: (128, 256)})
@@ -39,7 +38,7 @@ for _b in range(4):
 for _n in ("psc_", "pur", "py", "pk", "pd0", "pd1", "pd2", "pd3"):
     SCRATCH[_n] = ("psum", [128, 512], F32)
 
-SEMAPHORES = ["cV", "cP", "cS", "cG", "lp", "lx", "lu", "lw", "pad", "fin"]
+SEMAPHORES = ["cV", "cP", "cS", "cG", "lp", "lx", "lu", "lw", "fin"]
 SEMAPHORES += ["arr%d" % h for h in range(1, H + 1)] + ["snt%d" % h for h in range(H)] + ["st%d" % h for h in range(1, H + 1)]
 
 
@@ -49,9 +48,6 @@ def rank_program(g, core, T, topo):
         return
     n = len(T.cores)
     nxt, prv = T.cores[(rank + 1) % n], T.cores[(rank - 1) % n]
-
-    def lanes(a, b):
-        return topo.engines(a, b)[:8]
 
     queue = {"V": g.vector, "P": g.tensor, "S": g.scalar, "G": g, "Y": g.sync}
     cnt = {"V": 0, "P": 0, "S": 0, "G": 0}
@@ -135,8 +131,7 @@ def rank_program(g, core, T, topo):
 
     def send(h):
         rid, pid = topo.addr(nxt)[:2]
-        es = lanes(core, nxt)
-        mask = sum(1 << e for e in es)
+        mask = topo.mask(core, nxt)
         arr, snt = T.sem["arr%d" % (h + 1)], T.sem["snt%d" % h]
         before("G", ["p%d" % h], [], False)
         g.remote_dma(out_ap=T["w%d" % (h + 1)][:, 0:P].bitcast(dt.uint8), in_ap=T["p%d" % h][:, 0:P].bitcast(dt.uint8),
@@ -144,7 +139,7 @@ def rank_program(g, core, T, topo):
         before("G", ["q%d" % h], [], False)
         g.remote_dma(out_ap=T["v%d" % (h + 1)][:, 0:P], in_ap=T["q%d" % h][:, 0:P],
                      remote_sem=arr, local_sem=snt, pid=pid, routing_id=rid, dma_engine_mask=mask)
-        last["snt%d" % h] = 2 * len(es)
+        last["snt%d" % h] = 2 * len(topo.engines(core, nxt))
 
     dma("Y", T.tp[:, 0:256], T.pn[:], "lp", [], ["tp"])
     dma("S", T.tx[:], T.x[:], "lx", [], ["tx"])
@@ -157,28 +152,28 @@ def rank_program(g, core, T, topo):
     iota(T.i5[:], [[-16, 4]], 0, 1, "i5")
     iota(T.i6[:], [[0, 4]], 0, 1, "i6", False)
     iota(T.i7[:], [[16, 4]], 0, 0, "i7", False)
+    iota(T.i1[:], [[1, 128]], 0, -1, "i1")
+    iota(T.idx[:], [[8, C]], 68, 0, "idx")
 
     mset(T.tp[:, 256:512], 0.0, "tpz")
     mset(T.zero[:], 0.0, "zero")
     mset(T.kt[:, 0:64], 0.0, "kt")
     mset(T.xt[:], 0.0, "xt")
     mset(T.maskb[:], BIG, "maskb")
-    mset(T.bx[:], 0.0, "bx")
+    mset(T.bx[:], -1000.0, "bx")
     mset(T.cc[:, C:200], 4096.0, "ccx")
-    mset(T.ones[:], 1.0, "ones")
     mset(T.wide1[:], 0.0, "wide1")
-    mset(T.maskb[:, 0:16:5], 4.0, "maskb")
-    for (t, part, col, val) in ((T.kt, 64, 2, -256.0), (T.kt, 64, 3, 1.0), (T.kt, 96, 2, 1.0)):
-        op("V", lambda: V.memset(t[part:part + 1, col:64:4], val), ["kt"], ["kt%d%d" % (part, col)])
+    mset(T.maskb[:, 0:16:5], 0.5, "maskb")
+    for (part, col, val) in ((64, 2, -256.0), (64, 3, 1.0), (96, 2, 1.0)):
+        op("V", lambda: V.memset(T.kt[part:part + 1, col:64:4], val), ["kt"], ["kt%d%d" % (part, col)])
     for (part, a, b, val) in ((64, 2, 16, 1.0), (64, 18, 32, -0.25), (64, 19, 32, -8.0), (96, 18, 32, -0.5)):
         op("V", lambda: V.memset(T.xt[part:part + 1, a:b:4], val), ["xt"], ["xt%d%d" % (part, a)])
     xcon = ["xt", "xt642", "xt6418", "xt6419", "xt9618"]
     kcon = ["kt", "kt642", "kt643", "kt962"]
+    mset(T.z0[:], 0.0, "z0")
 
-    quant(T.p0[:], T.q0[:], T.tp[:], ["tp", "tpz"], ["p0", "q0"])
+    quant(T.p0[:, 0:128], T.q0[:, 0:128], T.tp[:], ["tp", "tpz"], ["p0", "q0"])
     send(0)
-    iota(T.i1[:], [[1, 128]], 0, -1, "i1")
-    iota(T.idx[:], [[8, C]], 68, 0, "idx")
     iota(T.vals[:], [[1, P]], C, 0, "vals")
     iota(T.win1[:], [[1, 256]], -64, 0, "win1")
 
@@ -199,7 +194,7 @@ def rank_program(g, core, T, topo):
     ts(T.wide1[:, 3:515:4], T.i1[:], 0.0, None, A.is_equal, None, ["i1"], ["wide1"])
     act(T.wide2[:], T.wide1[:], F.Copy, ["wide1"], ["wide2"], scale=-0.5)
     for k in (0, 32):
-        ts(T.tri[k:k + 32, :], T.i4[:], 0.0, None, A.is_gt, None, ["i4"], ["tri%d" % k])
+        ts(T.tri[k:k + 32, :], T.i4[:], 0.0, -1000.0, A.is_le, A.mult, ["i4"], ["tri%d" % k])
     ts(T.m4a[:], T.i5[:], 0.0, None, A.is_ge, None, ["i5"], ["m4a"])
     ts(T.m4b[:], T.i5[:], 16.0, None, A.is_lt, None, ["i5"], ["m4b"])
     ts(T.i6b[:], T.i6[:], 15, None, A.bitwise_and, None, ["i6"], ["i6b"])
@@ -210,6 +205,11 @@ def rank_program(g, core, T, topo):
     quant(T.kq[:], T.ks[:], T.kt[:], kcon, ["kq"])
     for b in range(4):
         quant(T["eq%d" % b][:], T["es%d" % b][:], T.wide1[:, 3 - b:515 - b], ["wide1"], ["eq%d" % b])
+
+    def pad(k):
+        quant(T["p%d" % k][:, 64:192], T["q%d" % k][:, 64:192], T.z0[:], ["z0"], ["pz%d" % k])
+
+    pad(1)
     mset(T.zt[:, 256:512], 0.0, "ztz")
 
     def urow(h):
@@ -220,7 +220,7 @@ def rank_program(g, core, T, topo):
         w, v, p, q = T["w%d" % h], T["v%d" % h], T["p%d" % h], T["q%d" % h]
         w2, v2 = T["w%d" % (h + 1)], T["v%d" % (h + 1)]
         off, tof, win = T["off%d" % h], T["tof%d" % h], T["win%d" % h]
-        got = 2 * len(lanes(prv, core))
+        got = 2 * len(topo.engines(prv, core))
         last["arr%d" % h] = got
         wa, wb, vb = "wa%d" % h, "wb%d" % h, "vb%d" % h
         res[wa] = {"w": ("arr%d" % h, got, {}), "r": []}
@@ -230,27 +230,20 @@ def rank_program(g, core, T, topo):
         for b in range(4):
             mm(T["pd%d" % b][:, 0:128], T["eq%d" % b][:], T["es%d" % b][:], w[:, 0:128], v[:, 0:128], pan + ["eq%d" % b], ["pd%d" % b], True, False)
         act(T.sgn[:], T.pur[0:64, 0:C], F.Sign, ["pur"], ["sgn"])
-        if h == 1:
-            for k in range(1, H + 1):
-                for (d, s, c) in ((T["p%d" % k][:, P:128].bitcast(dt.uint8), T.p0[:, P:128].bitcast(dt.uint8), "pz%d"), (T["q%d" % k][:, P:128], T.q0[:, P:128], "qz%d")):
-                    dma("Y", d, s, "pad", ["p0", wa], [c % k])
-            for k in range(1, H + 1):
-                for c in ("pz%d", "qz%d"):
-                    res[c % k] = {"w": ("pad", last["pad"], {}), "r": []}
         scan(T.rr[:], T.psc_[0:64, 0:C], T.zero[0:64, :], -1.0e29, A.max, A.add, ["psc_", "zero"], ["rr"])
+        act(T.less[:], T.rr[:], F.Sign, ["rr"], ["less", "pl"], bias=T.rr[:, C - 1:C], scale=-1.0, accum_out=T.pl[:])
         ts(T.lt[:], T.rr[:], T.rr[:, C - 1:C], 2048.0, A.is_lt, A.mult, ["rr"], ["lt"])
         scan(T.cc[:, 0:C], T.idx[:], T.sgn[:], 0.0, A.max, A.add, ["sgn", "idx"], ["cc"])
+        ts(T.bx[:, 32:64], T.tri[:], T.pl[:], None, A.add, None, ["tri0", "tri32", "pl"], ["bx"])
+        ts(T.bx[32:64, 0:32], T.zero[0:32, 0:32], T.pl[0:32, :], None, A.add, None, ["zero", "pl"], ["bx2"])
+        ts(T.tc[:], T.pl[:], 8.0, 68.0, A.mult, A.add, ["pl"], ["tc"])
         scan(T.vs[:], T.lt[:], T.cc[:, 1:C + 1], T.cc[:, 0:1], A.max, A.min, ["lt", "cc", "ccx"], ["vs"])
-        val = T.vs[:, C - 1:C]
-        ts(T.bx[:, 32:64], T.tri[:], val, None, A.mult, None, ["tri0", "tri32", "vs"], ["bx"])
-        ts(T.bx[32:64, 0:32], T.ones[:], val[0:32, :] if False else T.vs[0:32, C - 1:C], None, A.mult, None, ["ones", "vs"], ["bx2"])
-        ts(T.tc[:], val, M4, M4, A.add, A.subtract, ["vs"], ["tc"])
         op("V", lambda: V.transpose(T.by[:], T.bx[:]), ["bx", "bx2"], ["by"])
         ts(T.mm[64:128, :], T.mask4[:], T.tc[:], None, A.mult, None, ["mask4", "tc"], ["mm"])
-        ts(T.ne[:], T.by[:], val, None, A.subtract, None, ["by", "vs"], ["ne"])
-        ts(T.hb[:], T.tc[:], val, BIG, A.is_le, A.mult, ["tc", "vs"], ["hb"])
+        ts(T.ne[:], T.by[:], T.pl[:], None, A.not_equal, None, ["by", "pl"], ["ne"])
+        ts(T.hb[:], T.tc[:], T.vs[:, C - 1:C], BIG, A.is_le, A.mult, ["tc", "vs"], ["hb"])
         ts(T.xt[64:128, 16:32:4], T.mm[64:128, :], M128, M128, A.add, A.subtract, ["mm", "xt"], ["xhi"])
-        op("V", lambda: V.tensor_reduce(T.own[:], T.ne[:], AxisListType.X, A.min, apply_absolute_value=True), ["ne"], ["own"])
+        op("V", lambda: V.tensor_reduce(T.own[:], T.ne[:], AxisListType.X, A.min), ["ne"], ["own"])
         tt(T.xt[64:128, 17:32:4], T.mm[64:128, :], T.xt[64:128, 16:32:4], A.subtract, ["mm", "xhi"], ["xlo"])
         ts(T.xt[0:64, 0:16], T.maskb[:], T.hb[:], T.own[:], A.max, A.is_lt, ["maskb", "hb", "own", "xt"], ["xq_in"])
         quant(T.xq[:], T.xs[:], T.xt[:], xcon + ["xq_in", "xhi", "xlo"], ["xq"])
@@ -272,10 +265,10 @@ def rank_program(g, core, T, topo):
             tt(T.seg[:, 0:16], T.s1[:], T.s2[:], A.add, ["s1", "s2"], ["seg"])
             for (a, b) in ((16, 32), (32, 64), (64, 128), (128, 192)):
                 act(T.seg[:, a:b], T.seg[:, 0:b - a], F.Copy, ["seg"], ["seg"])
-        pq = ["p%d" % h, "q%d" % h, "pz%d" % h, "qz%d" % h]
+        pq = ["p%d" % h, "q%d" % h, "pz%d" % h]
         for b in (0, 2, 1, 3):
-            mm(T["pd%d" % b][:, 0:128], T["nq%d" % b][:], T["ns%d" % b][:], p[:], q[:], pq + ["nq%d" % b], ["pd%d" % b], False, True)
-        mm(T.py[:, 0:128], T.wq[:], T.ws[:], p[:], q[:], pq + ["wq"], ["py"])
+            mm(T["pd%d" % b][:, 0:128], T["nq%d" % b][:], T["ns%d" % b][:], p[:, 0:128], q[:, 0:128], pq + ["nq%d" % b], ["pd%d" % b], False, True)
+        mm(T.py[:, 0:128], T.wq[:], T.ws[:], p[:, 0:128], q[:, 0:128], pq + ["wq"], ["py"])
         op("V", lambda: V.tensor_copy(win[:].indirect(off[:, 0:4]), T.vals[:]), offs + ["vals", "win%d" % h], ["win%d" % h])
         scan(T.scn[:], T.seg[:], win[:, 64:256], 0.0, A.add, A.max, ["seg", "win%d" % h], ["scn"])
         for b in (0, 1):
@@ -290,6 +283,7 @@ def rank_program(g, core, T, topo):
         act(v2[:, 64:256], v[:, 64:384].indirect(tof[:, 0:12]), F.Copy, tab, ["vb%d" % (h + 1)])
         if h < H:
             urow(h + 1)
+            pad(h + 1)
         if h == 1:
             for k in range(2, H + 1):
                 iota(T["win%d" % k][:], [[1, 256]], -64, 0, "win%d" % k)

@@ -2,8 +2,8 @@ from concourse.bass import DstId, RemoteDMATransfer
 from concourse.mybir import dt, AluOpType as A, AxisListType, ActivationFunctionType as F
 
 P, C, H = 64, 192, 4
-BIG = 1.0e6
-M128 = 1.5 * 2.0 ** 30
+U0, T0, Z0, E0 = 64, 192, 384, 512
+BIG = 1.0e29
 F32, BF16, I32, U16, F8, U8 = "float32", "bfloat16", "int32", "uint16", "float8_e4m3fn_x4", "uint8"
 
 SCRATCH = {}
@@ -14,28 +14,32 @@ def _sb(dtype, **shapes):
         SCRATCH[name] = ("sbuf", list(shapes[name]), dtype)
 
 
-_sb(BF16, tp=(128, 512), tx=(128, 768), tw=(128, 512), tu=(128, 4), ur=(128, 768), nur=(128, 512), wide1=(128, 516), wide2=(128, 516),
-    kt=(128, 512), xt=(128, 512), zt=(128, 512), z0=(128, 512), vals=(128, P), sgn=(64, C), lt=(64, C), less=(64, C), ne=(64, 64))
-_sb(F32, zero=(128, C), i1=(128, 128), i2=(64, 64), k1=(64, 64), k2=(64, 64), i4=(32, 32), tri=(64, 32), i5=(64, 4),
-    m4a=(64, 4), m4b=(64, 4), mask4=(64, 4), islot=(128, 4), dcol=(128, 1), s1=(128, 16), s2=(128, 16), seg=(128, C), idx=(64, C),
-    maskb=(64, 16), cc=(64, 200), rr=(64, C), vs=(64, C), pl=(64, 1), tc=(64, 1), hb=(64, 1), own=(64, 1), bx=(64, 64), by=(64, 64),
-    mm=(128, 4), scn=(128, C), ys=(128, H * P))
+_sb(BF16, tp=(128, 512), tx=(128, 768), tw=(128, 512), tu=(128, 4), ur=(128, 512), wide1=(128, 516), wide2=(128, 516),
+    kt=(128, 512), xt=(128, 512), zt=(128, 512), z0=(128, 512), vals=(128, P), less=(128, C), less2=(128, 12), ne=(128, 96))
+_sb(F32, zero=(128, C), one=(128, 128), i2=(64, 64), k1=(64, 64), k2=(64, 64), tri=(64, 32), m4=(64, 4), mask4=(64, 4),
+    islot=(128, 4), dcol=(128, 1), s1=(128, 16), s2=(128, 16), seg=(128, C), offd=(128, 16), ud=(128, 16),
+    uw=(128, C), rr=(128, C), pl=(128, 1), hi=(128, 1), lo=(64, 1), bx=(64, 64), by=(64, 64), scn=(128, C),
+    dtw=(128, Z0), do3=(128, P), ys=(128, H * P))
 _sb(I32, i3=(128, 16), i3b=(128, 16), i6=(128, 4), i6b=(128, 4), i7=(128, 4))
-_sb(F8, urq=(128, C), nuq=(128, 128), wq=(128, 128), kq=(128, 128), xq=(128, 128))
-_sb(U8, urs=(128, C), nus=(128, 128), ws=(128, 128), ks=(128, 128), xs=(128, 128))
+_sb(F8, wq=(128, 128), kq=(128, 128), xq=(128, 128))
+_sb(U8, ws=(128, 128), ks=(128, 128), xs=(128, 128))
+_sb(U16, plu=(128, 2))
 for _h in range(1, H + 2):
-    _sb(F8, **{"w%d" % _h: (128, 384)})
-    _sb(U8, **{"v%d" % _h: (128, 384)})
+    _sb(F8, **{"w%d" % _h: (128, E0)})
+    _sb(U8, **{"v%d" % _h: (128, E0)})
 for _h in range(H + 1):
     _sb(F8, **{"p%d" % _h: (128, 192)})
     _sb(U8, **{"q%d" % _h: (128, 192)})
 for _h in range(1, H + 1):
     _sb(U16, **{"off%d" % _h: (128, 4), "tof%d" % _h: (128, 12)})
-    _sb(BF16, **{"win%d" % _h: (128, 256)})
+    _sb(BF16, **{"win%d" % _h: (128, Z0)})
 for _b in range(4):
-    _sb(F8, **{"eq%d" % _b: (128, 128), "nq%d" % _b: (128, 128)})
-    _sb(U8, **{"es%d" % _b: (128, 128), "ns%d" % _b: (128, 128)})
-for _n in ("psc_", "pur", "py", "pk", "pd0", "pd1", "pd2", "pd3"):
+    _sb(F8, **{"eq%d" % _b: (128, 128)})
+    _sb(U8, **{"es%d" % _b: (128, 128)})
+for _b in range(3):
+    _sb(F8, **{"nq%d" % _b: (128, 128)})
+    _sb(U8, **{"ns%d" % _b: (128, 128)})
+for _n in ("psc_", "pur", "pyk", "pd0", "pd1", "pd2", "pd3"):
     SCRATCH[_n] = ("psum", [128, 512], F32)
 
 SEMAPHORES = ["cV", "cP", "cS", "cG", "lp", "lx", "lu", "lw", "fin"]
@@ -99,8 +103,8 @@ def rank_program(g, core, T, topo):
 
     V, PE, S = g.vector, g.tensor, g.scalar
 
-    def mset(ap, c, w):
-        op("V", lambda: V.memset(ap, c), [], [w])
+    def mset(ap, c, w, reads=()):
+        op("V", lambda: V.memset(ap, c), list(reads), [w])
 
     def ts(out, in0, a, b, o0, o1, reads, writes):
         if b is None:
@@ -129,6 +133,17 @@ def rank_program(g, core, T, topo):
         else:
             op("G", lambda: g.iota(out, pat, base, cm), [], [w])
 
+    def select(out, in_, pat, cmp, fill, base, cm, reads, w):
+        op("G", lambda: g.affine_select(out, in_, pat, cmp, fill, base, cm), reads, [w])
+
+    def zeros(buf, cols, name):
+        names = []
+        for k in range(0, cols, C):
+            e = min(cols, k + C)
+            names.append("%s_%d" % (name, k))
+            act(T[buf][:, k:e], T.zero[:, 0:e - k], F.Copy, ["zero"], [names[-1]])
+        return names
+
     def send(h):
         rid, pid = topo.addr(nxt)[:2]
         mask = topo.mask(core, nxt)
@@ -146,155 +161,164 @@ def rank_program(g, core, T, topo):
     dma("Y", T.tu[:], T.u[:], "lu", [], ["tu"])
     dma("Y", T.tw[:], T.w[:], "lw", [], ["tw"])
 
+    mset(T.zero[:], 0.0, "zero")
+    mset(T.one[:], 1.0, "one")
     iota(T.i2[:], [[1, 16], [16, 4]], 0, -1, "i2")
     iota(T.i3[:], [[1, 16]], 0, -1, "i3", False)
-    iota(T.i4[:], [[1, 32]], 0, -1, "i4")
-    iota(T.i5[:], [[-16, 4]], 0, 1, "i5")
+    zw1 = zeros("wide1", 516, "wide1")
+    zxt = zeros("xt", 512, "xt")
+    select(T.tri[0:32, :], T.zero[0:32, 0:32], [[1, 32]], A.is_gt, -1000.0, 0, -1, ["zero"], "tri0")
+    select(T.tri[32:64, :], T.zero[32:64, 0:32], [[1, 32]], A.is_gt, -1000.0, 0, -1, ["zero", "tri0", "i3", "i2"], "tri32")
+    select(T.wide1[:, 3:515:4], T.one[:], [[1, 128]], A.is_equal, 0.0, 0, -1, ["one", "tri32"] + zw1, "wide1")
     iota(T.i6[:], [[0, 4]], 0, 1, "i6", False)
-    iota(T.i7[:], [[16, 4]], 0, 0, "i7", False)
-    iota(T.i1[:], [[1, 128]], 0, -1, "i1")
-    iota(T.idx[:], [[8, C]], 68, 0, "idx")
 
     mset(T.tp[:, 256:512], 0.0, "tpz")
-    mset(T.zero[:], 0.0, "zero")
     mset(T.kt[:, 0:64], 0.0, "kt")
-    mset(T.xt[:], 0.0, "xt")
-    mset(T.maskb[:], BIG, "maskb")
     mset(T.bx[:], -1000.0, "bx")
-    mset(T.cc[:, C:200], 4096.0, "ccx")
-    mset(T.wide1[:], 0.0, "wide1")
-    mset(T.maskb[:, 0:16:5], 0.5, "maskb")
-    for (part, col, val) in ((64, 2, -256.0), (64, 3, 1.0), (96, 2, 1.0)):
-        op("V", lambda: V.memset(T.kt[part:part + 1, col:64:4], val), ["kt"], ["kt%d%d" % (part, col)])
-    for (part, a, b, val) in ((64, 2, 16, 1.0), (64, 18, 32, -0.25), (64, 19, 32, -8.0), (96, 18, 32, -0.5)):
-        op("V", lambda: V.memset(T.xt[part:part + 1, a:b:4], val), ["xt"], ["xt%d%d" % (part, a)])
-    xcon = ["xt", "xt642", "xt6418", "xt6419", "xt9618"]
-    kcon = ["kt", "kt642", "kt643", "kt962"]
-    mset(T.z0[:], 0.0, "z0")
+    mset(T.kt[64:65, 2:64:4], -512.0, "kt2", ["kt"])
+    ts(T.k1[:], T.i2[:], 0.0, -1024.0, A.is_gt, A.mult, ["i2"], ["k1"])
+    ts(T.k2[:], T.i2[:], 0.0, 16384.0, A.is_equal, A.mult, ["i2"], ["k2"])
+    ts(T.i3b[:], T.i3[:], 15, None, A.bitwise_and, None, ["i3"], ["i3b"])
+    tt(T.kt[0:64, 0:64], T.k1[:], T.k2[:], A.add, ["k1", "k2", "kt"], ["ktl"])
+    for (t, val) in ((0, 16.0), (1, 1.0)):
+        ts(T.kt[64:128, t:64:4], T.i3b[64:128, :], 0, val, A.is_equal, A.mult, ["i3b", "kt"], ["kth%d" % t])
+    kcon = ["kt", "kt2", "ktl", "kth0", "kth1"]
 
     quant(T.p0[:, 0:128], T.q0[:, 0:128], T.tp[:], ["tp", "tpz"], ["p0", "q0"])
     send(0)
+    iota(T.i7[:], [[16, 4]], 0, 0, "i7", False)
+    select(T.m4[:], T.one[0:64, 0:4], [[-16, 4]], A.is_ge, 0.0, 0, 1, ["one"], "m4")
+    select(T.mask4[:], T.m4[:], [[16, 4]], A.is_ge, 0.0, 15, -1, ["m4"], "mask4")
     iota(T.vals[:], [[1, P]], C, 0, "vals")
-    iota(T.win1[:], [[1, 256]], -64, 0, "win1")
+    iota(T.win1[:, T0:Z0], [[1, C]], 0, 0, "win1")
 
+    quant(T.w1[:, T0:Z0], T.v1[:, T0:Z0], T.tx[:], ["tx"], ["wb1", "vb1"])
+    ts(T.s1[:], T.i3b[:], 0, -4000.0, A.is_equal, A.mult, ["i3b"], ["s1"])
+    ts(T.s2[:], T.i3b[:], 1, 1000.0, A.is_equal, A.mult, ["i3b"], ["s2"])
     for t in range(4):
-        act(T.ur[:, t:768:4], T.zero[:], F.Identity, ["zero", "tu"], ["ur%d" % t], bias=T.tu[:, t:t + 1])
-    act(T.nur[:], T.ur[:, 0:512], F.Copy, ["ur0", "ur1", "ur2", "ur3"], ["nur"], scale=-1.0)
-    quant(T.w1[:, 64:256], T.v1[:, 64:256], T.tx[:], ["tx"], ["wb1", "vb1"])
-    ts(T.k1[:], T.i2[:], 0.0, -512.0, A.is_gt, A.mult, ["i2"], ["k1"])
-    ts(T.k2[:], T.i2[:], 0.0, 8192.0, A.is_equal, A.mult, ["i2"], ["k2"])
-    ts(T.i3b[:], T.i3[:], 15, None, A.bitwise_and, None, ["i3"], ["i3b"])
-    tt(T.kt[0:64, 0:64], T.k1[:], T.k2[:], A.add, ["k1", "k2", "kt"], ["ktl"])
-    for t in range(2):
-        ts(T.kt[64:128, t:64:4], T.i3b[64:128, :], 0, 0.125, A.is_equal, A.mult, ["i3b", "kt"], ["kth%d" % t])
-    kcon += ["ktl", "kth0", "kth1"]
+        act(T.ur[:, t:512:4], T.zero[:, 0:128], F.Identity, ["zero", "tu"], ["ur%d" % t], bias=T.tu[:, t:t + 1])
     for k in (64, 128, 256):
         act(T.kt[:, k:2 * k], T.kt[:, 0:k], F.Copy, list(kcon), ["ktc%d" % k])
         kcon.append("ktc%d" % k)
-    ts(T.wide1[:, 3:515:4], T.i1[:], 0.0, None, A.is_equal, None, ["i1"], ["wide1"])
-    act(T.wide2[:], T.wide1[:], F.Copy, ["wide1"], ["wide2"], scale=-0.5)
-    for k in (0, 32):
-        ts(T.tri[k:k + 32, :], T.i4[:], 0.0, -1000.0, A.is_le, A.mult, ["i4"], ["tri%d" % k])
-    ts(T.m4a[:], T.i5[:], 0.0, None, A.is_ge, None, ["i5"], ["m4a"])
-    ts(T.m4b[:], T.i5[:], 16.0, None, A.is_lt, None, ["i5"], ["m4b"])
-    ts(T.i6b[:], T.i6[:], 15, None, A.bitwise_and, None, ["i6"], ["i6b"])
-    tt(T.mask4[:], T.m4a[:], T.m4b[:], A.mult, ["m4a", "m4b"], ["mask4"])
-    tt(T.islot[:], T.i6b[:], T.i7[:], A.add, ["i6b", "i7"], ["islot"])
-    quant(T.nuq[:], T.nus[:], T.nur[:], ["nur"], ["nuq"])
-    quant(T.urq[:], T.urs[:], T.ur[:], ["ur0", "ur1", "ur2", "ur3"], ["urq"])
-    quant(T.kq[:], T.ks[:], T.kt[:], kcon, ["kq"])
-    for b in range(4):
-        quant(T["eq%d" % b][:], T["es%d" % b][:], T.wide1[:, 3 - b:515 - b], ["wide1"], ["eq%d" % b])
+    for (a, b, val) in ((82, 96, 1.0), (98, 112, -0.375)):
+        mset(T.xt[64:65, a:b:4], val, "xtc%d" % a, zxt)
+    xcon = zxt + ["xtc82", "xtc98"]
+    mset(T.ne[:, 80:96], 1.0, "ne1")
+    tt(T.seg[:, 0:16], T.s1[:], T.s2[:], A.add, ["s1", "s2"], ["seg"])
+    for (a, b) in ((16, 32), (32, 64), (64, 128), (128, 192)):
+        act(T.seg[:, a:b], T.seg[:, 0:b - a], F.Copy, ["seg"], ["seg"])
+    zz0 = zeros("z0", 512, "z0")
+    ts(T.offd[:], T.i3b[:], 0, -BIG, A.not_equal, A.mult, ["i3b"], ["offd"])
+    mset(T.ne[:, 81:96:5], 2.0 ** -40, "ne2", ["ne1"])
+    mset(T.ne[:, 85:96:5], 2.0 ** 40, "ne3", ["ne1"])
+    ncon = ["ne1", "ne2", "ne3"]
+
+    def urep(k):
+        quant(T["w%d" % k][:, U0:T0], T["v%d" % k][:, U0:T0], T.ur[:], ["ur0", "ur1", "ur2", "ur3"], ["wu%d" % k])
+
+    def ones(b):
+        quant(T["eq%d" % b][:], T["es%d" % b][:], T.wide1[:, 3 - b:515 - b], zw1 + ["wide1"], ["eq%d" % b])
+
+    def halves(b):
+        quant(T["nq%d" % b][:], T["ns%d" % b][:], T.wide2[:, 3 - b:515 - b], ["wide2"], ["nq%d" % b])
 
     def pad(k):
-        quant(T["p%d" % k][:, 64:192], T["q%d" % k][:, 64:192], T.z0[:], ["z0"], ["pz%d" % k])
+        quant(T["p%d" % k][:, 64:192], T["q%d" % k][:, 64:192], T.z0[:], zz0, ["pz%d" % k])
 
-    pad(1)
-    mset(T.zt[:, 256:512], 0.0, "ztz")
+    urep(1)
+    ts(T.i6b[:], T.i6[:], 15, None, A.bitwise_and, None, ["i6"], ["i6b"])
+    quant(T.kq[:], T.ks[:], T.kt[:], kcon, ["kq"])
+    ts(T.dcol[:], T.i6b[:, 0:1], 14.5, 1000.0, A.is_lt, A.mult, ["i6b"], ["dcol"])
+    tt(T.islot[:], T.i6b[:], T.i7[:], A.add, ["i6b", "i7"], ["islot"])
+    ones(0)
+    ones(1)
 
-    def urow(h):
-        mm(T.pur[:, 0:C], T.nuq[:], T.nus[:], T["w%d" % h][:, 64:256], T["v%d" % h][:, 64:256], ["nuq", "wb%d" % h, "vb%d" % h], ["pur"], True, False)
-
-    urow(1)
     for h in range(1, H + 1):
         w, v, p, q = T["w%d" % h], T["v%d" % h], T["p%d" % h], T["q%d" % h]
         w2, v2 = T["w%d" % (h + 1)], T["v%d" % (h + 1)]
         off, tof, win = T["off%d" % h], T["tof%d" % h], T["win%d" % h]
         got = 2 * len(topo.engines(prv, core))
         last["arr%d" % h] = got
-        wa, wb, vb = "wa%d" % h, "wb%d" % h, "vb%d" % h
+        wa, wu, wb, vb = "wa%d" % h, "wu%d" % h, "wb%d" % h, "vb%d" % h
         res[wa] = {"w": ("arr%d" % h, got, {}), "r": []}
-        pan = [wa, wb, vb]
-        mm(T.psc_[:, 0:C], w[:, 0:128], v[:, 0:128], w[:, 64:256], v[:, 64:256], pan, ["psc_"])
-        mm(T.pur[:, 0:C], w[:, 0:128], v[:, 0:128], T.urq[:], T.urs[:], pan + ["urq"], ["pur"], False, True)
-        for b in range(4):
-            mm(T["pd%d" % b][:, 0:128], T["eq%d" % b][:], T["es%d" % b][:], w[:, 0:128], v[:, 0:128], pan + ["eq%d" % b], ["pd%d" % b], True, False)
-        act(T.sgn[:], T.pur[0:64, 0:C], F.Sign, ["pur"], ["sgn"])
-        scan(T.rr[:], T.psc_[0:64, 0:C], T.zero[0:64, :], -1.0e29, A.max, A.add, ["psc_", "zero"], ["rr"])
+        pan = [wa, wu, wb, vb]
+        mm(T.psc_[:, 0:C + 2], w[:, 0:128], v[:, 0:128], w[:, T0 - 2:Z0], v[:, T0 - 2:Z0], pan, ["psc_"])
+        mm(T.pur[:, 0:C], w[:, U0:T0], v[:, U0:T0], w[:, T0:Z0], v[:, T0:Z0], [wu, wb, vb], ["pur"])
+        scan(T.rr[:], T.psc_[:, 2:C + 2], T.zero[:], -BIG, A.max, A.add, ["psc_", "zero"], ["rr"])
         act(T.less[:], T.rr[:], F.Sign, ["rr"], ["less", "pl"], bias=T.rr[:, C - 1:C], scale=-1.0, accum_out=T.pl[:])
-        ts(T.lt[:], T.rr[:], T.rr[:, C - 1:C], 2048.0, A.is_lt, A.mult, ["rr"], ["lt"])
-        scan(T.cc[:, 0:C], T.idx[:], T.sgn[:], 0.0, A.max, A.add, ["sgn", "idx"], ["cc"])
-        ts(T.bx[:, 32:64], T.tri[:], T.pl[:], None, A.add, None, ["tri0", "tri32", "pl"], ["bx"])
-        ts(T.bx[32:64, 0:32], T.zero[0:32, 0:32], T.pl[0:32, :], None, A.add, None, ["zero", "pl"], ["bx2"])
-        ts(T.tc[:], T.pl[:], 8.0, 68.0, A.mult, A.add, ["pl"], ["tc"])
-        scan(T.vs[:], T.lt[:], T.cc[:, 1:C + 1], T.cc[:, 0:1], A.max, A.min, ["lt", "cc", "ccx"], ["vs"])
-        op("V", lambda: V.transpose(T.by[:], T.bx[:]), ["bx", "bx2"], ["by"])
-        ts(T.mm[64:128, :], T.mask4[:], T.tc[:], None, A.mult, None, ["mask4", "tc"], ["mm"])
-        ts(T.ne[:], T.by[:], T.pl[:], None, A.not_equal, None, ["by", "pl"], ["ne"])
-        ts(T.hb[:], T.tc[:], T.vs[:, C - 1:C], BIG, A.is_le, A.mult, ["tc", "vs"], ["hb"])
-        ts(T.xt[64:128, 16:32:4], T.mm[64:128, :], M128, M128, A.add, A.subtract, ["mm", "xt"], ["xhi"])
-        op("V", lambda: V.tensor_reduce(T.own[:], T.ne[:], AxisListType.X, A.min), ["ne"], ["own"])
-        tt(T.xt[64:128, 17:32:4], T.mm[64:128, :], T.xt[64:128, 16:32:4], A.subtract, ["mm", "xhi"], ["xlo"])
-        ts(T.xt[0:64, 0:16], T.maskb[:], T.hb[:], T.own[:], A.max, A.is_lt, ["maskb", "hb", "own", "xt"], ["xq_in"])
+        act(T.less2[:], T.rr[:, 15:C:16], F.Sign, ["rr"], ["less2", "hi"], bias=T.rr[:, C - 1:C], scale=-1.0, accum_out=T.hi[:])
+        ts(T.ud[:], T.offd[:], T.psc_[:, 0:1], None, A.add, None, ["offd", "psc_"], ["ud"])
+        if h == 1:
+            ones(2)
+            pad(1)
+        for b in range(3):
+            mm(T["pd%d" % b][:, 0:128], T["eq%d" % b][:], T["es%d" % b][:], w[:, 0:128], v[:, 0:128], pan + ["eq%d" % b], ["pd%d" % b], True, False)
+        act(T.uw[:], T.pur[:, 0:C], F.Copy, ["pur"], ["uw"])
+        act(T.lo[:], T.hi[0:64, :], F.Identity, ["hi", "pl"], ["lo"], scale=-16.0, bias=T.pl[0:64, :])
+        act(T.xt[64:128, 96:112:4], T.mask4[:], F.Copy, ["mask4", "hi"] + xcon, ["xhi"], scale=T.hi[0:64, :])
+        act(T.xt[64:128, 97:112:4], T.mask4[:], F.Copy, ["mask4", "lo"] + xcon, ["xlo"], scale=T.lo[:])
+        if h == 1:
+            act(T.wide2[:], T.wide1[:], F.Copy, zw1 + ["wide1"], ["wide2"], scale=-0.5)
+            act(T.dtw[:, 0:T0], T.zero[:], F.Copy, ["zero"], ["zdt"])
+            for k in (256, 384):
+                act(T.zt[:, k:k + 128], T.zero[:, 0:128], F.Copy, ["zero"], ["zzt%d" % k])
+        ts(T.bx[:, 32:64], T.tri[:], T.pl[0:64, :], None, A.add, None, ["tri0", "tri32", "pl", "bx"], ["bx1"])
+        ts(T.bx[32:64, 0:32], T.zero[0:32, 0:32], T.pl[0:32, :], None, A.add, None, ["zero", "pl", "bx"], ["bx2"])
+        op("V", lambda: V.tensor_copy(T.plu[:, 0:1], T.pl[:]), ["pl"], ["plu"])
+        op("V", lambda: V.transpose(T.by[:], T.bx[:]), ["bx", "bx1", "bx2"], ["by"])
+        op("V", lambda: V.tensor_tensor(T.ne[:, 64:80], T.uw[:].indirect(T.plu[:, 0:1]), T.ud[:], A.is_gt), ["plu", "uw", "ud"], ["neu"])
+        ts(T.ne[0:64, 0:64], T.by[:], T.pl[0:64, :], None, A.not_equal, None, ["by", "pl"], ["ne"])
+        scan(T.xt[0:64, 0:96], T.ne[0:64, :], T.zero[0:64, 0:96], 1.0, A.mult, A.add, ["ne", "neu", "zero"] + ncon + xcon, ["xq_in"])
         quant(T.xq[:], T.xs[:], T.xt[:], xcon + ["xq_in", "xhi", "xlo"], ["xq"])
-        mm(T.pk[:, 0:128], T.kq[:], T.ks[:], T.xq[:], T.xs[:], ["kq", "xq"], ["pk"])
+        mm(T.pyk[:, 0:128], T.kq[:], T.ks[:], T.xq[:], T.xs[:], ["kq", "xq"], ["pyk"])
+        if h == 1:
+            ones(3)
+            halves(0)
+        elif h < H:
+            urep(h + 1)
+        mm(T.pd3[:, 0:128], T.eq3[:], T.es3[:], w[:, 0:128], v[:, 0:128], pan + ["eq3"], ["pd3"])
+        mm(T.pur[:, 0:C], T.eq3[:], T.es3[:], w[:, T0:Z0], v[:, T0:Z0], [wb, vb, "eq3"], ["pur"])
         for c in range(4):
-            ts(off[:, c:c + 1], T.pk[:, c:c + 1], T.pk[:, 4 + c:5 + c], T.islot[:, c:c + 1], A.min, A.max, ["pk", "islot"], ["off%d_%d" % (h, c)])
+            ts(off[:, c:c + 1], T.pyk[:, 20 + c:21 + c], T.pyk[:, 24 + c:25 + c], T.islot[:, c:c + 1], A.min, A.max, ["pyk", "islot"], ["off%d_%d" % (h, c)])
         offs = ["off%d_%d" % (h, c) for c in range(4)]
-        op("V", lambda: V.tensor_copy(p[:, 0:P].bitcast(dt.uint32), w[:, 0:256].bitcast(dt.uint32).indirect(off[:, 0:4])), offs + pan, ["p%d" % h])
-        act(q[:, 0:P], v[:, 0:256].indirect(off[:, 0:4]), F.Copy, offs + pan, ["q%d" % h])
+        op("V", lambda: V.tensor_copy(p[:, 0:P].bitcast(dt.uint32), w[:, 0:Z0].bitcast(dt.uint32).indirect(off[:, 0:4])), offs + pan, ["p%d" % h])
+        act(q[:, 0:P], v[:, 0:Z0].indirect(off[:, 0:4]), F.Copy, offs + pan, ["q%d" % h])
         if h < H:
             send(h)
         if h == 1:
-            for b in range(4):
-                quant(T["nq%d" % b][:], T["ns%d" % b][:], T.wide2[:, 3 - b:515 - b], ["wide2"], ["nq%d" % b])
+            for b in (1, 2): halves(b)
             quant(T.wq[:], T.ws[:], T.tw[:], ["tw"], ["wq"])
-            ts(T.s1[:], T.i3b[:], 0, -4000.0, A.is_equal, A.mult, ["i3b"], ["s1"])
-            ts(T.s2[:], T.i3b[:], 1, 1000.0, A.is_equal, A.mult, ["i3b"], ["s2"])
-            ts(T.dcol[:], T.i6b[:, 0:1], 14.5, 1000.0, A.is_lt, A.mult, ["i6b"], ["dcol"])
-            tt(T.seg[:, 0:16], T.s1[:], T.s2[:], A.add, ["s1", "s2"], ["seg"])
-            for (a, b) in ((16, 32), (32, 64), (64, 128), (128, 192)):
-                act(T.seg[:, a:b], T.seg[:, 0:b - a], F.Copy, ["seg"], ["seg"])
         pq = ["p%d" % h, "q%d" % h, "pz%d" % h]
-        for b in (0, 2, 1, 3):
+        act(T.do3[:], T.pd3[:, 0:P], F.Copy, ["pd3"], ["do3"])
+        act(T.dtw[:, T0:Z0], T.pur[:, 0:C], F.Copy, ["pur"], ["dtw"], scale=-0.5)
+        for b in range(3):
             mm(T["pd%d" % b][:, 0:128], T["nq%d" % b][:], T["ns%d" % b][:], p[:, 0:128], q[:, 0:128], pq + ["nq%d" % b], ["pd%d" % b], False, True)
-        mm(T.py[:, 0:128], T.wq[:], T.ws[:], p[:, 0:128], q[:, 0:128], pq + ["wq"], ["py"])
+        mm(T.pyk[:, 0:128], T.wq[:], T.ws[:], p[:, 0:128], q[:, 0:128], pq + ["wq"], ["pyk"])
         op("V", lambda: V.tensor_copy(win[:].indirect(off[:, 0:4]), T.vals[:]), offs + ["vals", "win%d" % h], ["win%d" % h])
-        scan(T.scn[:], T.seg[:], win[:, 64:256], 0.0, A.add, A.max, ["seg", "win%d" % h], ["scn"])
-        for b in (0, 1):
-            op("V", lambda: V.tensor_copy(T.zt[:, b:256:4], T["pd%d" % b][:, 0:P]), ["pd%d" % b], ["zt%d" % b])
-        for b in (2, 3):
+        scan(T.scn[:], T.seg[:], win[:, T0:Z0], 0.0, A.add, A.max, ["seg", "win%d" % h], ["scn"])
+        op("V", lambda: V.tensor_tensor(T.zt[:, 3:256:4], T.dtw[:].indirect(off[:, 0:4]), T.do3[:], A.add), offs + ["zdt", "dtw", "do3"], ["zt3"])
+        for b in range(3):
             act(T.zt[:, b:256:4], T["pd%d" % b][:, 0:P], F.Copy, ["pd%d" % b], ["zt%d" % b])
         ts(tof[:], T.scn[:, 15:C:16], T.dcol[:], None, A.subtract, None, ["scn", "dcol"], ["tof%d" % h])
-        quant(w[:, 256:384], v[:, 256:384], T.zt[:], ["zt0", "zt1", "zt2", "zt3", "ztz"], ["wz%d" % h])
-        act(T.ys[:, (h - 1) * P:h * P], T.py[:, 0:P], F.Copy, ["py"], ["ys%d" % h])
+        quant(w[:, Z0:E0], v[:, Z0:E0], T.zt[:], ["zt0", "zt1", "zt2", "zt3", "zzt256", "zzt384"], ["wz%d" % h])
+        act(T.ys[:, (h - 1) * P:h * P], T.pyk[:, 0:P], F.Copy, ["pyk"], ["ys%d" % h])
         tab = [wb, vb, "wz%d" % h, "tof%d" % h]
-        op("V", lambda: V.tensor_copy(w2[:, 64:256].bitcast(dt.uint32), w[:, 64:384].bitcast(dt.uint32).indirect(tof[:, 0:12])), tab, ["wb%d" % (h + 1)])
-        act(v2[:, 64:256], v[:, 64:384].indirect(tof[:, 0:12]), F.Copy, tab, ["vb%d" % (h + 1)])
+        op("V", lambda: V.tensor_copy(w2[:, T0:Z0].bitcast(dt.uint32), w[:, T0:E0].bitcast(dt.uint32).indirect(tof[:, 0:12])), tab, ["wb%d" % (h + 1)])
+        act(v2[:, T0:Z0], v[:, T0:E0].indirect(tof[:, 0:12]), F.Copy, tab, ["vb%d" % (h + 1)])
+        if h == 1: urep(2)
         if h < H:
-            urow(h + 1)
             pad(h + 1)
         if h == 1:
             for k in range(2, H + 1):
-                iota(T["win%d" % k][:], [[1, 256]], -64, 0, "win%d" % k)
+                iota(T["win%d" % k][:, T0:Z0], [[1, C]], 0, 0, "win%d" % k)
         if h == H:
             dma("Y", T.pc[:], p[:, 0:P].bitcast(dt.uint8), "fin", ["p%d" % h], [])
             for k in range(4):
                 dma("Y", T.psc[4 * k:4 * k + 4, :], q[32 * k:32 * k + 4, 0:P], "fin", ["q%d" % h], [])
         dma("Y", T.y[:, (h - 1) * P:h * P], T.ys[:, (h - 1) * P:h * P], "st%d" % h, ["ys%d" % h], [])
     e = H + 1
-    dma("Y", T.oc[:], T["w%d" % e][:, 64:256].bitcast(dt.uint8), "fin", ["wb%d" % e], [])
+    dma("Y", T.oc[:], T["w%d" % e][:, T0:Z0].bitcast(dt.uint8), "fin", ["wb%d" % e], [])
     for k in range(4):
-        dma("S" if k % 2 else "Y", T.osc[4 * k:4 * k + 4, :], T["v%d" % e][32 * k:32 * k + 4, 64:256], "fin", ["vb%d" % e], [])
+        dma("S" if k % 2 else "Y", T.osc[4 * k:4 * k + 4, :], T["v%d" % e][32 * k:32 * k + 4, T0:Z0], "fin", ["vb%d" % e], [])
     for sem in sorted(last):
         need("G", (sem, last[sem], {}))

@@ -15,31 +15,28 @@ def _sb(dtype, **shapes):
 
 
 _sb(BF16, tp=(128, 512), tx=(128, 768), tw=(128, 512), tu=(128, 4), ur=(128, 512), wide1=(128, 516), wide2=(128, 516),
-    kt=(128, 512), xt=(128, 512), zt=(128, 512), z0=(128, 512), vals=(128, P), less=(128, C), less2=(128, 12), ne=(128, 96))
+    kt=(128, 512), xt=(128, 512), xl=(128, 512), zt=(128, 512), z0=(128, 512), vals=(128, P), less=(128, 16 + C),
+    less2=(128, 13), ne=(128, 96), zb=(128, 96), seg=(128, C), s1=(128, 16), s2=(128, 16), scn=(128, C))
 _sb(F32, zero=(128, C), one=(128, 128), i2=(64, 64), k1=(64, 64), k2=(64, 64), tri=(64, 32), m4=(64, 4), mask4=(64, 4),
-    islot=(128, 4), dcol=(128, 1), s1=(128, 16), s2=(128, 16), seg=(128, C), offd=(128, 16), ud=(128, 16),
-    uw=(128, C), rr=(128, C), pl=(128, 1), hi=(128, 1), lo=(64, 1), bx=(64, 64), by=(64, 64), scn=(128, C),
-    dtw=(128, Z0), do3=(128, P), ys=(128, H * P))
+    km=(64, 4), islot=(128, 4), dcol=(128, 1), offd=(128, 16), ud=(128, 16), uw=(128, 16 + C), rr=(128, 16 + C), pl=(128, 1),
+    hi=(128, 1), bx=(64, 64), by=(64, 64), ys=(128, H * P))
 _sb(I32, i3=(128, 16), i3b=(128, 16), i6=(128, 4), i6b=(128, 4), i7=(128, 4))
-_sb(F8, wq=(128, 128), kq=(128, 128), xq=(128, 128))
-_sb(U8, ws=(128, 128), ks=(128, 128), xs=(128, 128))
+_sb(F8, wq=(128, 128), kq=(128, 128), xq=(128, 128), lq=(128, 128))
+_sb(U8, ws=(128, 128), ks=(128, 128), xs=(128, 128), ls=(128, 128))
 _sb(U16, plu=(128, 2))
 for _h in range(1, H + 2):
     _sb(F8, **{"w%d" % _h: (128, E0)})
     _sb(U8, **{"v%d" % _h: (128, E0)})
 for _h in range(H + 1):
-    _sb(F8, **{"p%d" % _h: (128, 192)})
-    _sb(U8, **{"q%d" % _h: (128, 192)})
+    _sb(F8, **{"p%d" % _h: (128, 256)})
+    _sb(U8, **{"q%d" % _h: (128, 256)})
 for _h in range(1, H + 1):
-    _sb(U16, **{"off%d" % _h: (128, 4), "tof%d" % _h: (128, 12)})
+    _sb(U16, **{"off%d" % _h: (128, 4), "lp%d" % _h: (128, 4), "tof%d" % _h: (128, 12)})
     _sb(BF16, **{"win%d" % _h: (128, Z0)})
 for _b in range(4):
-    _sb(F8, **{"eq%d" % _b: (128, 128)})
-    _sb(U8, **{"es%d" % _b: (128, 128)})
-for _b in range(3):
-    _sb(F8, **{"nq%d" % _b: (128, 128)})
-    _sb(U8, **{"ns%d" % _b: (128, 128)})
-for _n in ("psc_", "pur", "pyk", "pd0", "pd1", "pd2", "pd3"):
+    _sb(F8, **{"eq%d" % _b: (128, 128), "nq%d" % _b: (128, 128)})
+    _sb(U8, **{"es%d" % _b: (128, 128), "ns%d" % _b: (128, 128)})
+for _n in ("psc_", "pur", "pyk", "ppl", "pd0", "pd1", "pd2", "pd3"):
     SCRATCH[_n] = ("psum", [128, 512], F32)
 
 SEMAPHORES = ["cV", "cP", "cS", "cG", "lp", "lx", "lu", "lw", "fin"]
@@ -115,6 +112,9 @@ def rank_program(g, core, T, topo):
     def tt(out, a, b, o, reads, writes):
         op("V", lambda: V.tensor_tensor(out, a, b, o), reads, writes)
 
+    def cp(out, in_, reads, writes):
+        op("V", lambda: V.tensor_copy(out, in_), reads, writes)
+
     def scan(out, a, b, init, o0, o1, reads, writes):
         op("V", lambda: V.tensor_tensor_scan(out, a, b, init, o0, o1), reads, writes)
 
@@ -127,19 +127,19 @@ def rank_program(g, core, T, topo):
     def act(out, in_, f, reads, writes, **kw):
         op("S", lambda: S.activation(out, in_, f, **kw), reads, writes)
 
-    def iota(out, pat, base, cm, w, flag=True):
+    def iota(out, pat, base, cm, w, flag=True, reads=()):
         if flag:
-            op("G", lambda: g.iota(out, pat, base, cm, allow_small_or_imprecise_dtypes=True), [], [w])
+            op("G", lambda: g.iota(out, pat, base, cm, allow_small_or_imprecise_dtypes=True), list(reads), [w])
         else:
-            op("G", lambda: g.iota(out, pat, base, cm), [], [w])
+            op("G", lambda: g.iota(out, pat, base, cm), list(reads), [w])
 
     def select(out, in_, pat, cmp, fill, base, cm, reads, w):
         op("G", lambda: g.affine_select(out, in_, pat, cmp, fill, base, cm), reads, [w])
 
-    def zeros(buf, cols, name):
+    def zeros(buf, name):
         names = []
-        for k in range(0, cols, C):
-            e = min(cols, k + C)
+        for k in range(0, 512, C):
+            e = min(512, k + C)
             names.append("%s_%d" % (name, k))
             act(T[buf][:, k:e], T.zero[:, 0:e - k], F.Copy, ["zero"], [names[-1]])
         return names
@@ -148,10 +148,10 @@ def rank_program(g, core, T, topo):
         rid, pid = topo.addr(nxt)[:2]
         mask = topo.mask(core, nxt)
         arr, snt = T.sem["arr%d" % (h + 1)], T.sem["snt%d" % h]
-        before("G", ["p%d" % h], [], False)
+        before("G", ["p%d" % h, "p_%d" % h], [], False)
         g.remote_dma(out_ap=T["w%d" % (h + 1)][:, 0:P].bitcast(dt.uint8), in_ap=T["p%d" % h][:, 0:P].bitcast(dt.uint8),
                      remote_sem=arr, local_sem=snt, pid=pid, routing_id=rid, dma_engine_mask=mask)
-        before("G", ["q%d" % h], [], False)
+        before("G", ["q%d" % h, "q_%d" % h], [], False)
         g.remote_dma(out_ap=T["v%d" % (h + 1)][:, 0:P], in_ap=T["q%d" % h][:, 0:P],
                      remote_sem=arr, local_sem=snt, pid=pid, routing_id=rid, dma_engine_mask=mask)
         last["snt%d" % h] = 2 * len(topo.engines(core, nxt))
@@ -163,80 +163,89 @@ def rank_program(g, core, T, topo):
 
     mset(T.zero[:], 0.0, "zero")
     mset(T.one[:], 1.0, "one")
+    mset(T.wide1[:], 0.0, "wide1z")
     iota(T.i2[:], [[1, 16], [16, 4]], 0, -1, "i2")
     iota(T.i3[:], [[1, 16]], 0, -1, "i3", False)
-    zw1 = zeros("wide1", 516, "wide1")
-    zxt = zeros("xt", 512, "xt")
-    select(T.tri[0:32, :], T.zero[0:32, 0:32], [[1, 32]], A.is_gt, -1000.0, 0, -1, ["zero"], "tri0")
-    select(T.tri[32:64, :], T.zero[32:64, 0:32], [[1, 32]], A.is_gt, -1000.0, 0, -1, ["zero", "tri0", "i3", "i2"], "tri32")
-    select(T.wide1[:, 3:515:4], T.one[:], [[1, 128]], A.is_equal, 0.0, 0, -1, ["one", "tri32"] + zw1, "wide1")
     iota(T.i6[:], [[0, 4]], 0, 1, "i6", False)
+    select(T.wide1[:, 3:515:4], T.one[:], [[1, 128]], A.is_equal, 0.0, 0, -1, ["one", "wide1z"], "wide1")
+    select(T.tri[0:32, :], T.zero[0:32, 0:32], [[1, 32]], A.is_gt, -1000.0, 0, -1, ["zero"], "tri0")
+    zxt = zeros("xt", "xt")
+    zxl = zeros("xl", "xl")
 
     mset(T.tp[:, 256:512], 0.0, "tpz")
     mset(T.kt[:, 0:64], 0.0, "kt")
-    mset(T.bx[:], -1000.0, "bx")
-    mset(T.kt[64:65, 2:64:4], -512.0, "kt2", ["kt"])
     ts(T.k1[:], T.i2[:], 0.0, -1024.0, A.is_gt, A.mult, ["i2"], ["k1"])
     ts(T.k2[:], T.i2[:], 0.0, 16384.0, A.is_equal, A.mult, ["i2"], ["k2"])
     ts(T.i3b[:], T.i3[:], 15, None, A.bitwise_and, None, ["i3"], ["i3b"])
+    mset(T.kt[64:65, 2:64:4], -512.0, "kt2", ["kt"])
     tt(T.kt[0:64, 0:64], T.k1[:], T.k2[:], A.add, ["k1", "k2", "kt"], ["ktl"])
     for (t, val) in ((0, 16.0), (1, 1.0)):
         ts(T.kt[64:128, t:64:4], T.i3b[64:128, :], 0, val, A.is_equal, A.mult, ["i3b", "kt"], ["kth%d" % t])
     kcon = ["kt", "kt2", "ktl", "kth0", "kth1"]
+    ts(T.s1[:], T.i3b[:], 0, None, A.not_equal, None, ["i3b"], ["s1"])
+    ts(T.s2[:], T.i3b[:], 1, 1023.0, A.is_equal, A.mult, ["i3b"], ["s2"])
+    ts(T.i6b[:], T.i6[:], 15, None, A.bitwise_and, None, ["i6"], ["i6b"])
 
     quant(T.p0[:, 0:128], T.q0[:, 0:128], T.tp[:], ["tp", "tpz"], ["p0", "q0"])
     send(0)
-    iota(T.i7[:], [[16, 4]], 0, 0, "i7", False)
+    select(T.tri[32:64, :], T.zero[32:64, 0:32], [[1, 32]], A.is_gt, -1000.0, 0, -1, ["zero", "tri0", "wide1", "i6", "i3", "i2"], "tri32")
+    iota(T.i7[:], [[16, 4]], 0, 0, "i7", False, ["tri32"])
     select(T.m4[:], T.one[0:64, 0:4], [[-16, 4]], A.is_ge, 0.0, 0, 1, ["one"], "m4")
     select(T.mask4[:], T.m4[:], [[16, 4]], A.is_ge, 0.0, 15, -1, ["m4"], "mask4")
-    iota(T.vals[:], [[1, P]], C, 0, "vals")
-    iota(T.win1[:, T0:Z0], [[1, C]], 0, 0, "win1")
-
-    quant(T.w1[:, T0:Z0], T.v1[:, T0:Z0], T.tx[:], ["tx"], ["wb1", "vb1"])
-    ts(T.s1[:], T.i3b[:], 0, -4000.0, A.is_equal, A.mult, ["i3b"], ["s1"])
-    ts(T.s2[:], T.i3b[:], 1, 1000.0, A.is_equal, A.mult, ["i3b"], ["s2"])
-    for t in range(4):
-        act(T.ur[:, t:512:4], T.zero[:, 0:128], F.Identity, ["zero", "tu"], ["ur%d" % t], bias=T.tu[:, t:t + 1])
-    for k in (64, 128, 256):
-        act(T.kt[:, k:2 * k], T.kt[:, 0:k], F.Copy, list(kcon), ["ktc%d" % k])
-        kcon.append("ktc%d" % k)
-    for (a, b, val) in ((82, 96, 1.0), (98, 112, -0.375)):
-        mset(T.xt[64:65, a:b:4], val, "xtc%d" % a, zxt)
-    xcon = zxt + ["xtc82", "xtc98"]
-    mset(T.ne[:, 80:96], 1.0, "ne1")
-    tt(T.seg[:, 0:16], T.s1[:], T.s2[:], A.add, ["s1", "s2"], ["seg"])
-    for (a, b) in ((16, 32), (32, 64), (64, 128), (128, 192)):
-        act(T.seg[:, a:b], T.seg[:, 0:b - a], F.Copy, ["seg"], ["seg"])
-    zz0 = zeros("z0", 512, "z0")
-    ts(T.offd[:], T.i3b[:], 0, -BIG, A.not_equal, A.mult, ["i3b"], ["offd"])
-    mset(T.ne[:, 81:96:5], 2.0 ** -40, "ne2", ["ne1"])
-    mset(T.ne[:, 85:96:5], 2.0 ** 40, "ne3", ["ne1"])
-    ncon = ["ne1", "ne2", "ne3"]
+    iota(T.z0[:], [[0, 512]], 0, 0, "z0")
+    iota(T.vals[:], [[1, P]], C + 1, 0, "vals")
+    iota(T.win1[:, T0:Z0], [[1, C]], 1, 0, "win1")
 
     def urep(k):
         quant(T["w%d" % k][:, U0:T0], T["v%d" % k][:, U0:T0], T.ur[:], ["ur0", "ur1", "ur2", "ur3"], ["wu%d" % k])
 
     def ones(b):
-        quant(T["eq%d" % b][:], T["es%d" % b][:], T.wide1[:, 3 - b:515 - b], zw1 + ["wide1"], ["eq%d" % b])
+        quant(T["eq%d" % b][:], T["es%d" % b][:], T.wide1[:, 3 - b:515 - b], ["wide1z", "wide1"], ["eq%d" % b])
 
     def halves(b):
         quant(T["nq%d" % b][:], T["ns%d" % b][:], T.wide2[:, 3 - b:515 - b], ["wide2"], ["nq%d" % b])
 
-    def pad(k):
-        quant(T["p%d" % k][:, 64:192], T["q%d" % k][:, 64:192], T.z0[:], zz0, ["pz%d" % k])
+    def pad(k, z=T.z0, names=("z0",)):
+        quant(T["p%d" % k][:, 128:256], T["q%d" % k][:, 128:256], z[:], list(names), ["pz%d" % k])
 
-    urep(1)
-    ts(T.i6b[:], T.i6[:], 15, None, A.bitwise_and, None, ["i6"], ["i6b"])
-    quant(T.kq[:], T.ks[:], T.kt[:], kcon, ["kq"])
-    ts(T.dcol[:], T.i6b[:, 0:1], 14.5, 1000.0, A.is_lt, A.mult, ["i6b"], ["dcol"])
-    tt(T.islot[:], T.i6b[:], T.i7[:], A.add, ["i6b", "i7"], ["islot"])
+    for t in range(4):
+        act(T.ur[:, t:512:4], T.zero[:, 0:128], F.Identity, ["zero", "tu"], ["ur%d" % t], bias=T.tu[:, t:t + 1])
+    tt(T.seg[:, 0:16], T.s1[:], T.s2[:], A.add, ["s1", "s2"], ["seg"])
+    for k in (64, 128, 256):
+        act(T.kt[:, k:2 * k], T.kt[:, 0:k], F.Copy, list(kcon), ["ktc%d" % k])
+        kcon.append("ktc%d" % k)
+        act(T.seg[:, k // 4:k // 2], T.seg[:, 0:k // 4], F.Copy, ["seg"], ["seg"])
+    act(T.zt[:, 256:384], T.zero[:, 0:128], F.Copy, ["zero"], ["zzt256"])
+    act(T.seg[:, 128:192], T.seg[:, 0:64], F.Copy, ["seg"], ["seg"])
+    act(T.zt[:, 384:512], T.zero[:, 0:128], F.Copy, ["zero"], ["zzt384"])
+    act(T.wide2[:], T.wide1[:], F.Copy, ["wide1z", "wide1"], ["wide2"], scale=-0.5)
+    act(T.km[:], T.mask4[:], F.Copy, ["mask4"], ["km"], scale=984.0, bias=-1000.0)
+
     ones(0)
     ones(1)
+    ones(2)
+    pad(1, T.xt, zxt)
+    quant(T.w1[:, T0:Z0], T.v1[:, T0:Z0], T.tx[:], ["tx"], ["wb1", "vb1"])
+    urep(1)
+    mset(T.ne[:, 80:96], 1.0, "ne1")
+    mset(T.bx[:], -1000.0, "bx")
+    mset(T.rr[:, 0:16], -BIG, "rr0")
+    mset(T.uw[:, 0:16], 0.0, "uw0")
+    mset(T.xt[64:65, 82:96:4], 1.0, "xtc", zxt + ["pz1"])
+    mset(T.xl[64:65, 2:16:4], -0.34375, "xlc", zxl)
+    xcon, lcon = zxt + ["xtc"], zxl + ["xlc"]
+    ts(T.offd[:], T.i3b[:], 0, -BIG, A.not_equal, A.mult, ["i3b"], ["offd"])
+    ones(3)
+    quant(T.kq[:], T.ks[:], T.kt[:], kcon, ["kq"])
+    mset(T.zb[:], 0.0, "zb")
+    mset(T.ne[:, 81:96:5], 2.0 ** -40, "ne2", ["ne1"])
+    mset(T.ne[:, 85:96:5], 2.0 ** 40, "ne3", ["ne1"])
+    ncon = ["ne1", "ne2", "ne3"]
 
     for h in range(1, H + 1):
         w, v, p, q = T["w%d" % h], T["v%d" % h], T["p%d" % h], T["q%d" % h]
         w2, v2 = T["w%d" % (h + 1)], T["v%d" % (h + 1)]
-        off, tof, win = T["off%d" % h], T["tof%d" % h], T["win%d" % h]
+        off, lp, tof, win = T["off%d" % h], T["lp%d" % h], T["tof%d" % h], T["win%d" % h]
         got = 2 * len(topo.engines(prv, core))
         last["arr%d" % h] = got
         wa, wu, wb, vb = "wa%d" % h, "wu%d" % h, "wb%d" % h, "vb%d" % h
@@ -244,81 +253,84 @@ def rank_program(g, core, T, topo):
         pan = [wa, wu, wb, vb]
         mm(T.psc_[:, 0:C + 2], w[:, 0:128], v[:, 0:128], w[:, T0 - 2:Z0], v[:, T0 - 2:Z0], pan, ["psc_"])
         mm(T.pur[:, 0:C], w[:, U0:T0], v[:, U0:T0], w[:, T0:Z0], v[:, T0:Z0], [wu, wb, vb], ["pur"])
-        scan(T.rr[:], T.psc_[:, 2:C + 2], T.zero[:], -BIG, A.max, A.add, ["psc_", "zero"], ["rr"])
-        act(T.less[:], T.rr[:], F.Sign, ["rr"], ["less", "pl"], bias=T.rr[:, C - 1:C], scale=-1.0, accum_out=T.pl[:])
-        act(T.less2[:], T.rr[:, 15:C:16], F.Sign, ["rr"], ["less2", "hi"], bias=T.rr[:, C - 1:C], scale=-1.0, accum_out=T.hi[:])
+        scan(T.rr[:, 16:], T.psc_[:, 2:C + 2], T.zero[:], -BIG, A.max, A.add, ["psc_", "zero"], ["rr"])
+        act(T.less[:], T.rr[:], F.Sign, ["rr", "rr0"], ["less", "pl"], bias=T.rr[:, 15 + C:16 + C], scale=-1.0, accum_out=T.pl[:])
+        act(T.less2[:], T.rr[:, 15:16 + C:16], F.Sign, ["rr", "rr0"], ["less2", "hi"], bias=T.rr[:, 15 + C:16 + C], scale=-1.0, accum_out=T.hi[:])
         ts(T.ud[:], T.offd[:], T.psc_[:, 0:1], None, A.add, None, ["offd", "psc_"], ["ud"])
-        if h == 1:
-            ones(2)
-            pad(1)
-        for b in range(3):
+        for b in range(4):
             mm(T["pd%d" % b][:, 0:128], T["eq%d" % b][:], T["es%d" % b][:], w[:, 0:128], v[:, 0:128], pan + ["eq%d" % b], ["pd%d" % b], True, False)
-        act(T.uw[:], T.pur[:, 0:C], F.Copy, ["pur"], ["uw"])
-        act(T.lo[:], T.hi[0:64, :], F.Identity, ["hi", "pl"], ["lo"], scale=-16.0, bias=T.pl[0:64, :])
-        act(T.xt[64:128, 96:112:4], T.mask4[:], F.Copy, ["mask4", "hi"] + xcon, ["xhi"], scale=T.hi[0:64, :])
-        act(T.xt[64:128, 97:112:4], T.mask4[:], F.Copy, ["mask4", "lo"] + xcon, ["xlo"], scale=T.lo[:])
+        cp(T.uw[:, 16:], T.pur[:, 0:C], ["pur"], ["uw"])
         if h == 1:
-            act(T.wide2[:], T.wide1[:], F.Copy, zw1 + ["wide1"], ["wide2"], scale=-0.5)
-            act(T.dtw[:, 0:T0], T.zero[:], F.Copy, ["zero"], ["zdt"])
-            for k in (256, 384):
-                act(T.zt[:, k:k + 128], T.zero[:, 0:128], F.Copy, ["zero"], ["zzt%d" % k])
+            halves(0)
+            halves(1)
+        act(T.bx[32:64, 0:32], T.zero[0:32, 0:32], F.Identity, ["zero", "pl", "bx"], ["bx2"], bias=T.pl[0:32, :])
         ts(T.bx[:, 32:64], T.tri[:], T.pl[0:64, :], None, A.add, None, ["tri0", "tri32", "pl", "bx"], ["bx1"])
-        ts(T.bx[32:64, 0:32], T.zero[0:32, 0:32], T.pl[0:32, :], None, A.add, None, ["zero", "pl", "bx"], ["bx2"])
-        op("V", lambda: V.tensor_copy(T.plu[:, 0:1], T.pl[:]), ["pl"], ["plu"])
+        cp(T.plu[:, 0:1], T.pl[:], ["pl"], ["plu"])
+        act(T.xl[64:128, 0:16:4], T.mask4[:], F.Copy, ["mask4", "hi"] + lcon, ["xhi"], scale=T.hi[0:64, :])
+        act(T.xl[64:128, 1:16:4], T.km[:], F.Relu, ["km", "hi", "pl"] + lcon, ["xlo"], scale=T.hi[0:64, :], bias=T.pl[0:64, :])
         op("V", lambda: V.transpose(T.by[:], T.bx[:]), ["bx", "bx1", "bx2"], ["by"])
-        op("V", lambda: V.tensor_tensor(T.ne[:, 64:80], T.uw[:].indirect(T.plu[:, 0:1]), T.ud[:], A.is_gt), ["plu", "uw", "ud"], ["neu"])
+        op("V", lambda: V.tensor_tensor(T.ne[:, 64:80], T.uw[:].indirect(T.plu[:, 0:1]), T.ud[:], A.is_gt), ["plu", "uw", "uw0", "ud"], ["neu"])
         ts(T.ne[0:64, 0:64], T.by[:], T.pl[0:64, :], None, A.not_equal, None, ["by", "pl"], ["ne"])
-        scan(T.xt[0:64, 0:96], T.ne[0:64, :], T.zero[0:64, 0:96], 1.0, A.mult, A.add, ["ne", "neu", "zero"] + ncon + xcon, ["xq_in"])
-        quant(T.xq[:], T.xs[:], T.xt[:], xcon + ["xq_in", "xhi", "xlo"], ["xq"])
+        quant(T.lq[:], T.ls[:], T.xl[:], lcon + ["xhi", "xlo"], ["lq"])
+        mm(T.ppl[:, 0:128], T.kq[:], T.ks[:], T.lq[:], T.ls[:], ["kq", "lq"], ["ppl"])
+        scan(T.xt[0:64, 0:96], T.ne[0:64, :], T.zb[0:64, :], 1.0, A.mult, A.add, ["ne", "neu", "zb"] + ncon + xcon, ["xq_in"])
+        if h == 1:
+            halves(2)
+        quant(T.xq[:], T.xs[:], T.xt[:], xcon + ["xq_in"], ["xq"])
         mm(T.pyk[:, 0:128], T.kq[:], T.ks[:], T.xq[:], T.xs[:], ["kq", "xq"], ["pyk"])
         if h == 1:
-            ones(3)
-            halves(0)
-        elif h < H:
-            urep(h + 1)
-        mm(T.pd3[:, 0:128], T.eq3[:], T.es3[:], w[:, 0:128], v[:, 0:128], pan + ["eq3"], ["pd3"])
-        mm(T.pur[:, 0:C], T.eq3[:], T.es3[:], w[:, T0:Z0], v[:, T0:Z0], [wb, vb, "eq3"], ["pur"])
+            tt(T.islot[:], T.i6b[:], T.i7[:], A.add, ["i6b", "i7"], ["islot"])
+        cp(lp[:], T.ppl[:, 0:4], ["ppl"], ["lp%d" % h])
+        if h == 1:
+            halves(3)
+        lps = ["lp%d" % h] + pan
+        cp(p[:, 64:128].bitcast(dt.uint32), w[:, 0:Z0].bitcast(dt.uint32).indirect(lp[:, 0:4]), lps, ["pe%d" % h])
+        act(q[:, 64:128], v[:, 0:Z0].indirect(lp[:, 0:4]), F.Copy, lps, ["qe%d" % h])
+        ent = ["pe%d" % h, "qe%d" % h, "pz%d" % h]
+        for b in range(4):
+            mm(T["pd%d" % b][:, 0:128], T["nq%d" % b][:], T["ns%d" % b][:], p[:, 64:192], q[:, 64:192], ent + ["nq%d" % b], ["pd%d" % b], False, True)
         for c in range(4):
-            ts(off[:, c:c + 1], T.pyk[:, 20 + c:21 + c], T.pyk[:, 24 + c:25 + c], T.islot[:, c:c + 1], A.min, A.max, ["pyk", "islot"], ["off%d_%d" % (h, c)])
+            ts(off[:, c:c + 1], T.pyk[:, 20 + c:21 + c], T.ppl[:, c:c + 1], T.islot[:, c:c + 1], A.min, A.max, ["pyk", "ppl", "islot"], ["off%d_%d" % (h, c)])
         offs = ["off%d_%d" % (h, c) for c in range(4)]
-        op("V", lambda: V.tensor_copy(p[:, 0:P].bitcast(dt.uint32), w[:, 0:Z0].bitcast(dt.uint32).indirect(off[:, 0:4])), offs + pan, ["p%d" % h])
-        act(q[:, 0:P], v[:, 0:Z0].indirect(off[:, 0:4]), F.Copy, offs + pan, ["q%d" % h])
+        for (a, b, i) in ((0, 2, "_"), (2, 4, "")):
+            cp(p[:, 16 * a:16 * b].bitcast(dt.uint32), w[:, 0:Z0].bitcast(dt.uint32).indirect(off[:, a:b]), offs[a:b] + pan, ["p%s%d" % (i, h)])
+            act(q[:, 16 * a:16 * b], v[:, 0:Z0].indirect(off[:, a:b]), F.Copy, offs[a:b] + pan, ["q%s%d" % (i, h)])
+        pqs = [c + i + "%d" % h for c in "pq" for i in ("_", "")]
         if h < H:
             send(h)
+        cp(win[:].indirect(off[:, 0:4]), T.vals[:], offs + ["vals", "win%d" % h], ["win%d" % h])
         if h == 1:
-            for b in (1, 2): halves(b)
-            quant(T.wq[:], T.ws[:], T.tw[:], ["tw"], ["wq"])
-        pq = ["p%d" % h, "q%d" % h, "pz%d" % h]
-        act(T.do3[:], T.pd3[:, 0:P], F.Copy, ["pd3"], ["do3"])
-        act(T.dtw[:, T0:Z0], T.pur[:, 0:C], F.Copy, ["pur"], ["dtw"], scale=-0.5)
-        for b in range(3):
-            mm(T["pd%d" % b][:, 0:128], T["nq%d" % b][:], T["ns%d" % b][:], p[:, 0:128], q[:, 0:128], pq + ["nq%d" % b], ["pd%d" % b], False, True)
-        mm(T.pyk[:, 0:128], T.wq[:], T.ws[:], p[:, 0:128], q[:, 0:128], pq + ["wq"], ["pyk"])
-        op("V", lambda: V.tensor_copy(win[:].indirect(off[:, 0:4]), T.vals[:]), offs + ["vals", "win%d" % h], ["win%d" % h])
-        scan(T.scn[:], T.seg[:], win[:, T0:Z0], 0.0, A.add, A.max, ["seg", "win%d" % h], ["scn"])
-        op("V", lambda: V.tensor_tensor(T.zt[:, 3:256:4], T.dtw[:].indirect(off[:, 0:4]), T.do3[:], A.add), offs + ["zdt", "dtw", "do3"], ["zt3"])
-        for b in range(3):
+            ts(T.dcol[:], T.i6b[:, 0:1], 15.0, 2.0 ** -10, A.is_ge, A.max, ["i6b"], ["dcol"])
+        for b in range(4):
             act(T.zt[:, b:256:4], T["pd%d" % b][:, 0:P], F.Copy, ["pd%d" % b], ["zt%d" % b])
-        ts(tof[:], T.scn[:, 15:C:16], T.dcol[:], None, A.subtract, None, ["scn", "dcol"], ["tof%d" % h])
+        scan(T.scn[:], T.seg[:], win[:, T0:Z0], 0.0, A.mult, A.max, ["seg", "win%d" % h], ["scn"])
+        if h == 1:
+            quant(T.wq[:], T.ws[:], T.tw[:], ["tw"], ["wq"])
         quant(w[:, Z0:E0], v[:, Z0:E0], T.zt[:], ["zt0", "zt1", "zt2", "zt3", "zzt256", "zzt384"], ["wz%d" % h])
+        ts(tof[:], T.scn[:, 15:C:16], T.dcol[:], -1.0, A.mult, A.add, ["scn", "dcol"], ["tof%d" % h])
+        mm(T.pyk[:, 0:128], T.wq[:], T.ws[:], p[:, 0:128], q[:, 0:128], pqs + ent + ["wq"], ["pyk"])
         act(T.ys[:, (h - 1) * P:h * P], T.pyk[:, 0:P], F.Copy, ["pyk"], ["ys%d" % h])
         tab = [wb, vb, "wz%d" % h, "tof%d" % h]
-        op("V", lambda: V.tensor_copy(w2[:, T0:Z0].bitcast(dt.uint32), w[:, T0:E0].bitcast(dt.uint32).indirect(tof[:, 0:12])), tab, ["wb%d" % (h + 1)])
-        act(v2[:, T0:Z0], v[:, T0:E0].indirect(tof[:, 0:12]), F.Copy, tab, ["vb%d" % (h + 1)])
+        for (a, b, i) in (((0, 6, "_"), (6, 12, "")) if h == H else ((0, 12, ""),)):
+            l, r = T0 + 16 * a, T0 + 16 * b
+            cp(w2[:, l:r].bitcast(dt.uint32), w[:, T0:E0].bitcast(dt.uint32).indirect(tof[:, a:b]), tab, ["wb%s%d" % (i, h + 1)])
+            act(v2[:, l:r], v[:, T0:E0].indirect(tof[:, a:b]), F.Copy, tab, ["vb%s%d" % (i, h + 1)])
         if h == 1: urep(2)
         if h < H:
             pad(h + 1)
+            if h + 2 <= H: urep(h + 2)
         if h == 1:
             for k in range(2, H + 1):
-                iota(T["win%d" % k][:, T0:Z0], [[1, C]], 0, 0, "win%d" % k)
+                iota(T["win%d" % k][:, T0:Z0], [[1, C]], 1, 0, "win%d" % k)
         if h == H:
-            dma("Y", T.pc[:], p[:, 0:P].bitcast(dt.uint8), "fin", ["p%d" % h], [])
+            dma("Y", T.pc[:], p[:, 0:P].bitcast(dt.uint8), "fin", ["p%d" % h, "p_%d" % h], [])
             for k in range(4):
-                dma("Y", T.psc[4 * k:4 * k + 4, :], q[32 * k:32 * k + 4, 0:P], "fin", ["q%d" % h], [])
+                dma("Y", T.psc[4 * k:4 * k + 4, :], q[32 * k:32 * k + 4, 0:P], "fin", ["q%d" % h, "q_%d" % h], [])
         dma("Y", T.y[:, (h - 1) * P:h * P], T.ys[:, (h - 1) * P:h * P], "st%d" % h, ["ys%d" % h], [])
     e = H + 1
-    dma("Y", T.oc[:], T["w%d" % e][:, T0:Z0].bitcast(dt.uint8), "fin", ["wb%d" % e], [])
+    for (a, b, i) in ((0, 6, "_"), (6, 12, "")):
+        dma("Y", T.oc[:, 64 * a:64 * b], T["w%d" % e][:, T0 + 16 * a:T0 + 16 * b].bitcast(dt.uint8), "fin", ["wb%s%d" % (i, e)], [])
     for k in range(4):
-        dma("S" if k % 2 else "Y", T.osc[4 * k:4 * k + 4, :], T["v%d" % e][32 * k:32 * k + 4, T0:Z0], "fin", ["vb%d" % e], [])
+        dma("S" if k % 2 else "Y", T.osc[4 * k:4 * k + 4, :], T["v%d" % e][32 * k:32 * k + 4, T0:Z0], "fin", ["vb_%d" % e, "vb%d" % e], [])
     for sem in sorted(last):
         need("G", (sem, last[sem], {}))

from concourse.bass import DstId, RemoteDMATransfer
from concourse.mybir import dt, AluOpType as A, AxisListType, ActivationFunctionType as F

P, C, H = 64, 192, 4
U0, T0, Z0, E0 = 64, 192, 384, 512
BIG = 1.0e29
F32, BF16, I32, U16, F8, U8 = "float32", "bfloat16", "int32", "uint16", "float8_e4m3fn_x4", "uint8"

SCRATCH = {}


def _sb(dtype, **shapes):
    for name in shapes:
        SCRATCH[name] = ("sbuf", list(shapes[name]), dtype)


_sb(BF16, tp=(128, 512), tx=(128, 768), tw=(128, 512), tu=(128, 4), ur=(128, 512), wide1=(128, 516), wide2=(128, 516),
    kt=(128, 512), xt=(128, 512), xl=(128, 512), zt=(128, 512), z0=(128, 512), vals=(128, P), less=(128, 16 + C),
    less2=(128, 13), ne=(128, 96), zb=(128, 96), seg=(128, C), s1=(128, 16), s2=(128, 16), scn=(128, C))
_sb(F32, zero=(128, C), one=(128, 128), i2=(64, 64), k1=(64, 64), k2=(64, 64), tri=(64, 32), m4=(64, 4), mask4=(64, 4),
    km=(64, 4), islot=(128, 4), dcol=(128, 1), offd=(128, 16), ud=(128, 16), uw=(128, 16 + C), rr=(128, 16 + C), pl=(128, 1),
    hi=(128, 1), bx=(64, 64), by=(64, 64), ys=(128, H * P))
_sb(I32, i3=(128, 16), i3b=(128, 16), i6=(128, 4), i6b=(128, 4), i7=(128, 4))
_sb(F8, wq=(128, 128), kq=(128, 128), xq=(128, 128), lq=(128, 128))
_sb(U8, ws=(128, 128), ks=(128, 128), xs=(128, 128), ls=(128, 128))
_sb(U16, plu=(128, 2))
for _h in range(1, H + 2):
    _sb(F8, **{"w%d" % _h: (128, E0)})
    _sb(U8, **{"v%d" % _h: (128, E0)})
for _h in range(H + 1):
    _sb(F8, **{"p%d" % _h: (128, 256)})
    _sb(U8, **{"q%d" % _h: (128, 256)})
for _h in range(1, H + 1):
    _sb(U16, **{"off%d" % _h: (128, 4), "lp%d" % _h: (128, 4), "tof%d" % _h: (128, 12)})
    _sb(BF16, **{"win%d" % _h: (128, Z0)})
for _b in range(4):
    _sb(F8, **{"eq%d" % _b: (128, 128), "nq%d" % _b: (128, 128)})
    _sb(U8, **{"es%d" % _b: (128, 128), "ns%d" % _b: (128, 128)})
for _n in ("psc_", "pur", "pyk", "ppl", "pd0", "pd1", "pd2", "pd3"):
    SCRATCH[_n] = ("psum", [128, 512], F32)

SEMAPHORES = ["cV", "cP", "cS", "cG", "lp", "lx", "lu", "lw", "fin"]
SEMAPHORES += ["arr%d" % h for h in range(1, H + 1)] + ["snt%d" % h for h in range(H)] + ["st%d" % h for h in range(1, H + 1)]


def rank_program(g, core, T, topo):
    rank = T.rank_of(core)
    if rank is None:
        return
    n = len(T.cores)
    nxt, prv = T.cores[(rank + 1) % n], T.cores[(rank - 1) % n]

    queue = {"V": g.vector, "P": g.tensor, "S": g.scalar, "G": g, "Y": g.sync}
    cnt = {"V": 0, "P": 0, "S": 0, "G": 0}
    known = {e: {} for e in queue}
    res = {}
    last = {}

    def need(e, dep):
        sem, val, clock = dep
        if known[e].get(sem, 0) >= val:
            return
        queue[e].wait_ge(T.sem[sem], val)
        known[e][sem] = val
        for k, v in clock.items():
            if known[e].get(k, 0) < v:
                known[e][k] = v

    def before(e, reads, writes, nowaw):
        deps = []
        for r in reads:
            if r in res and res[r]["w"]: deps.append(res[r]["w"])
        for w in writes:
            if w in res:
                if res[w]["w"] and not nowaw: deps.append(res[w]["w"])
                deps += [d for (f, d) in res[w]["r"] if f != e]
        for d in sorted(deps, key=lambda d: -d[1]):
            need(e, d)

    def after(e, reads, writes, dep):
        for r in reads:
            res.setdefault(r, {"w": None, "r": []})["r"].append((e, dep))
        for w in writes:
            res[w] = {"w": dep, "r": []}

    def op(e, call, reads, writes, nowaw=False):
        before(e, reads, writes, nowaw)
        i = call()
        cnt[e] += 1
        sem = "c" + e
        i.then_inc(T.sem[sem], 1)
        last[sem] = cnt[e]
        after(e, reads, writes, (sem, cnt[e], dict(known[e])))

    def dma(e, out, in_, sem, reads, writes):
        before(e, reads, writes, False)
        queue[e].dma_start(out, in_).then_inc(T.sem[sem], 16)
        last[sem] = last.get(sem, 0) + 16
        after(e, reads, writes, (sem, last[sem], dict(known[e])))

    V, PE, S = g.vector, g.tensor, g.scalar

    def mset(ap, c, w, reads=()):
        op("V", lambda: V.memset(ap, c), list(reads), [w])

    def ts(out, in0, a, b, o0, o1, reads, writes):
        if b is None:
            op("V", lambda: V.tensor_scalar(out, in0, a, None, o0), reads, writes)
        else:
            op("V", lambda: V.tensor_scalar(out, in0, a, b, o0, o1), reads, writes)

    def tt(out, a, b, o, reads, writes):
        op("V", lambda: V.tensor_tensor(out, a, b, o), reads, writes)

    def cp(out, in_, reads, writes):
        op("V", lambda: V.tensor_copy(out, in_), reads, writes)

    def scan(out, a, b, init, o0, o1, reads, writes):
        op("V", lambda: V.tensor_tensor_scan(out, a, b, init, o0, o1), reads, writes)

    def quant(q, s, t, reads, writes):
        op("V", lambda: V.quantize_mx(q, s, t), reads, writes)

    def mm(out, l, ls, r, rs, reads, writes, start=True, stop=True):
        op("P", lambda: PE.matmul_mx(out, l, ls, r, rs, start, stop), reads, writes, nowaw=not start)

    def act(out, in_, f, reads, writes, **kw):
        op("S", lambda: S.activation(out, in_, f, **kw), reads, writes)

    def iota(out, pat, base, cm, w, flag=True, reads=()):
        if flag:
            op("G", lambda: g.iota(out, pat, base, cm, allow_small_or_imprecise_dtypes=True), list(reads), [w])
        else:
            op("G", lambda: g.iota(out, pat, base, cm), list(reads), [w])

    def select(out, in_, pat, cmp, fill, base, cm, reads, w):
        op("G", lambda: g.affine_select(out, in_, pat, cmp, fill, base, cm), reads, [w])

    def zeros(buf, name):
        names = []
        for k in range(0, 512, C):
            e = min(512, k + C)
            names.append("%s_%d" % (name, k))
            act(T[buf][:, k:e], T.zero[:, 0:e - k], F.Copy, ["zero"], [names[-1]])
        return names

    def send(h):
        rid, pid = topo.addr(nxt)[:2]
        mask = topo.mask(core, nxt)
        arr, snt = T.sem["arr%d" % (h + 1)], T.sem["snt%d" % h]
        before("G", ["p%d" % h, "p_%d" % h], [], False)
        g.remote_dma(out_ap=T["w%d" % (h + 1)][:, 0:P].bitcast(dt.uint8), in_ap=T["p%d" % h][:, 0:P].bitcast(dt.uint8),
                     remote_sem=arr, local_sem=snt, pid=pid, routing_id=rid, dma_engine_mask=mask)
        before("G", ["q%d" % h, "q_%d" % h], [], False)
        g.remote_dma(out_ap=T["v%d" % (h + 1)][:, 0:P], in_ap=T["q%d" % h][:, 0:P],
                     remote_sem=arr, local_sem=snt, pid=pid, routing_id=rid, dma_engine_mask=mask)
        last["snt%d" % h] = 2 * len(topo.engines(core, nxt))

    dma("Y", T.tp[:, 0:256], T.pn[:], "lp", [], ["tp"])
    dma("S", T.tx[:], T.x[:], "lx", [], ["tx"])
    dma("Y", T.tu[:], T.u[:], "lu", [], ["tu"])
    dma("Y", T.tw[:], T.w[:], "lw", [], ["tw"])

    mset(T.zero[:], 0.0, "zero")
    mset(T.one[:], 1.0, "one")
    mset(T.wide1[:], 0.0, "wide1z")
    iota(T.i2[:], [[1, 16], [16, 4]], 0, -1, "i2")
    iota(T.i3[:], [[1, 16]], 0, -1, "i3", False)
    iota(T.i6[:], [[0, 4]], 0, 1, "i6", False)
    select(T.wide1[:, 3:515:4], T.one[:], [[1, 128]], A.is_equal, 0.0, 0, -1, ["one", "wide1z"], "wide1")
    select(T.tri[0:32, :], T.zero[0:32, 0:32], [[1, 32]], A.is_gt, -1000.0, 0, -1, ["zero"], "tri0")
    zxt = zeros("xt", "xt")
    zxl = zeros("xl", "xl")

    mset(T.tp[:, 256:512], 0.0, "tpz")
    mset(T.kt[:, 0:64], 0.0, "kt")
    ts(T.k1[:], T.i2[:], 0.0, -1024.0, A.is_gt, A.mult, ["i2"], ["k1"])
    ts(T.k2[:], T.i2[:], 0.0, 16384.0, A.is_equal, A.mult, ["i2"], ["k2"])
    ts(T.i3b[:], T.i3[:], 15, None, A.bitwise_and, None, ["i3"], ["i3b"])
    mset(T.kt[64:65, 2:64:4], -512.0, "kt2", ["kt"])
    tt(T.kt[0:64, 0:64], T.k1[:], T.k2[:], A.add, ["k1", "k2", "kt"], ["ktl"])
    for (t, val) in ((0, 16.0), (1, 1.0)):
        ts(T.kt[64:128, t:64:4], T.i3b[64:128, :], 0, val, A.is_equal, A.mult, ["i3b", "kt"], ["kth%d" % t])
    kcon = ["kt", "kt2", "ktl", "kth0", "kth1"]
    ts(T.s1[:], T.i3b[:], 0, None, A.not_equal, None, ["i3b"], ["s1"])
    ts(T.s2[:], T.i3b[:], 1, 1023.0, A.is_equal, A.mult, ["i3b"], ["s2"])
    ts(T.i6b[:], T.i6[:], 15, None, A.bitwise_and, None, ["i6"], ["i6b"])

    quant(T.p0[:, 0:128], T.q0[:, 0:128], T.tp[:], ["tp", "tpz"], ["p0", "q0"])
    send(0)
    select(T.tri[32:64, :], T.zero[32:64, 0:32], [[1, 32]], A.is_gt, -1000.0, 0, -1, ["zero", "tri0", "wide1", "i6", "i3", "i2"], "tri32")
    iota(T.i7[:], [[16, 4]], 0, 0, "i7", False, ["tri32"])
    select(T.m4[:], T.one[0:64, 0:4], [[-16, 4]], A.is_ge, 0.0, 0, 1, ["one"], "m4")
    select(T.mask4[:], T.m4[:], [[16, 4]], A.is_ge, 0.0, 15, -1, ["m4"], "mask4")
    iota(T.z0[:], [[0, 512]], 0, 0, "z0")
    iota(T.vals[:], [[1, P]], C + 1, 0, "vals")
    iota(T.win1[:, T0:Z0], [[1, C]], 1, 0, "win1")

    def urep(k):
        quant(T["w%d" % k][:, U0:T0], T["v%d" % k][:, U0:T0], T.ur[:], ["ur0", "ur1", "ur2", "ur3"], ["wu%d" % k])

    def ones(b):
        quant(T["eq%d" % b][:], T["es%d" % b][:], T.wide1[:, 3 - b:515 - b], ["wide1z", "wide1"], ["eq%d" % b])

    def halves(b):
        quant(T["nq%d" % b][:], T["ns%d" % b][:], T.wide2[:, 3 - b:515 - b], ["wide2"], ["nq%d" % b])

    def pad(k, z=T.z0, names=("z0",)):
        quant(T["p%d" % k][:, 128:256], T["q%d" % k][:, 128:256], z[:], list(names), ["pz%d" % k])

    for t in range(4):
        act(T.ur[:, t:512:4], T.zero[:, 0:128], F.Identity, ["zero", "tu"], ["ur%d" % t], bias=T.tu[:, t:t + 1])
    tt(T.seg[:, 0:16], T.s1[:], T.s2[:], A.add, ["s1", "s2"], ["seg"])
    for k in (64, 128, 256):
        act(T.kt[:, k:2 * k], T.kt[:, 0:k], F.Copy, list(kcon), ["ktc%d" % k])
        kcon.append("ktc%d" % k)
        act(T.seg[:, k // 4:k // 2], T.seg[:, 0:k // 4], F.Copy, ["seg"], ["seg"])
    act(T.zt[:, 256:384], T.zero[:, 0:128], F.Copy, ["zero"], ["zzt256"])
    act(T.seg[:, 128:192], T.seg[:, 0:64], F.Copy, ["seg"], ["seg"])
    act(T.zt[:, 384:512], T.zero[:, 0:128], F.Copy, ["zero"], ["zzt384"])
    act(T.wide2[:], T.wide1[:], F.Copy, ["wide1z", "wide1"], ["wide2"], scale=-0.5)
    act(T.km[:], T.mask4[:], F.Copy, ["mask4"], ["km"], scale=984.0, bias=-1000.0)

    ones(0)
    ones(1)
    ones(2)
    pad(1, T.xt, zxt)
    quant(T.w1[:, T0:Z0], T.v1[:, T0:Z0], T.tx[:], ["tx"], ["wb1", "vb1"])
    urep(1)
    mset(T.ne[:, 80:96], 1.0, "ne1")
    mset(T.bx[:], -1000.0, "bx")
    mset(T.rr[:, 0:16], -BIG, "rr0")
    mset(T.uw[:, 0:16], 0.0, "uw0")
    mset(T.xt[64:65, 82:96:4], 1.0, "xtc", zxt + ["pz1"])
    mset(T.xl[64:65, 2:16:4], -0.34375, "xlc", zxl)
    xcon, lcon = zxt + ["xtc"], zxl + ["xlc"]
    ts(T.offd[:], T.i3b[:], 0, -BIG, A.not_equal, A.mult, ["i3b"], ["offd"])
    ones(3)
    quant(T.kq[:], T.ks[:], T.kt[:], kcon, ["kq"])
    mset(T.zb[:], 0.0, "zb")
    mset(T.ne[:, 81:96:5], 2.0 ** -40, "ne2", ["ne1"])
    mset(T.ne[:, 85:96:5], 2.0 ** 40, "ne3", ["ne1"])
    ncon = ["ne1", "ne2", "ne3"]

    for h in range(1, H + 1):
        w, v, p, q = T["w%d" % h], T["v%d" % h], T["p%d" % h], T["q%d" % h]
        w2, v2 = T["w%d" % (h + 1)], T["v%d" % (h + 1)]
        off, lp, tof, win = T["off%d" % h], T["lp%d" % h], T["tof%d" % h], T["win%d" % h]
        got = 2 * len(topo.engines(prv, core))
        last["arr%d" % h] = got
        wa, wu, wb, vb = "wa%d" % h, "wu%d" % h, "wb%d" % h, "vb%d" % h
        res[wa] = {"w": ("arr%d" % h, got, {}), "r": []}
        pan = [wa, wu, wb, vb]
        mm(T.psc_[:, 0:C + 2], w[:, 0:128], v[:, 0:128], w[:, T0 - 2:Z0], v[:, T0 - 2:Z0], pan, ["psc_"])
        mm(T.pur[:, 0:C], w[:, U0:T0], v[:, U0:T0], w[:, T0:Z0], v[:, T0:Z0], [wu, wb, vb], ["pur"])
        scan(T.rr[:, 16:], T.psc_[:, 2:C + 2], T.zero[:], -BIG, A.max, A.add, ["psc_", "zero"], ["rr"])
        act(T.less[:], T.rr[:], F.Sign, ["rr", "rr0"], ["less", "pl"], bias=T.rr[:, 15 + C:16 + C], scale=-1.0, accum_out=T.pl[:])
        act(T.less2[:], T.rr[:, 15:16 + C:16], F.Sign, ["rr", "rr0"], ["less2", "hi"], bias=T.rr[:, 15 + C:16 + C], scale=-1.0, accum_out=T.hi[:])
        ts(T.ud[:], T.offd[:], T.psc_[:, 0:1], None, A.add, None, ["offd", "psc_"], ["ud"])
        for b in range(4):
            mm(T["pd%d" % b][:, 0:128], T["eq%d" % b][:], T["es%d" % b][:], w[:, 0:128], v[:, 0:128], pan + ["eq%d" % b], ["pd%d" % b], True, False)
        cp(T.uw[:, 16:], T.pur[:, 0:C], ["pur"], ["uw"])
        if h == 1:
            halves(0)
            halves(1)
        act(T.bx[32:64, 0:32], T.zero[0:32, 0:32], F.Identity, ["zero", "pl", "bx"], ["bx2"], bias=T.pl[0:32, :])
        ts(T.bx[:, 32:64], T.tri[:], T.pl[0:64, :], None, A.add, None, ["tri0", "tri32", "pl", "bx"], ["bx1"])
        cp(T.plu[:, 0:1], T.pl[:], ["pl"], ["plu"])
        act(T.xl[64:128, 0:16:4], T.mask4[:], F.Copy, ["mask4", "hi"] + lcon, ["xhi"], scale=T.hi[0:64, :])
        act(T.xl[64:128, 1:16:4], T.km[:], F.Relu, ["km", "hi", "pl"] + lcon, ["xlo"], scale=T.hi[0:64, :], bias=T.pl[0:64, :])
        op("V", lambda: V.transpose(T.by[:], T.bx[:]), ["bx", "bx1", "bx2"], ["by"])
        op("V", lambda: V.tensor_tensor(T.ne[:, 64:80], T.uw[:].indirect(T.plu[:, 0:1]), T.ud[:], A.is_gt), ["plu", "uw", "uw0", "ud"], ["neu"])
        ts(T.ne[0:64, 0:64], T.by[:], T.pl[0:64, :], None, A.not_equal, None, ["by", "pl"], ["ne"])
        quant(T.lq[:], T.ls[:], T.xl[:], lcon + ["xhi", "xlo"], ["lq"])
        mm(T.ppl[:, 0:128], T.kq[:], T.ks[:], T.lq[:], T.ls[:], ["kq", "lq"], ["ppl"])
        scan(T.xt[0:64, 0:96], T.ne[0:64, :], T.zb[0:64, :], 1.0, A.mult, A.add, ["ne", "neu", "zb"] + ncon + xcon, ["xq_in"])
        if h == 1:
            halves(2)
        quant(T.xq[:], T.xs[:], T.xt[:], xcon + ["xq_in"], ["xq"])
        mm(T.pyk[:, 0:128], T.kq[:], T.ks[:], T.xq[:], T.xs[:], ["kq", "xq"], ["pyk"])
        if h == 1:
            tt(T.islot[:], T.i6b[:], T.i7[:], A.add, ["i6b", "i7"], ["islot"])
        cp(lp[:], T.ppl[:, 0:4], ["ppl"], ["lp%d" % h])
        if h == 1:
            halves(3)
        lps = ["lp%d" % h] + pan
        cp(p[:, 64:128].bitcast(dt.uint32), w[:, 0:Z0].bitcast(dt.uint32).indirect(lp[:, 0:4]), lps, ["pe%d" % h])
        act(q[:, 64:128], v[:, 0:Z0].indirect(lp[:, 0:4]), F.Copy, lps, ["qe%d" % h])
        ent = ["pe%d" % h, "qe%d" % h, "pz%d" % h]
        for b in range(4):
            mm(T["pd%d" % b][:, 0:128], T["nq%d" % b][:], T["ns%d" % b][:], p[:, 64:192], q[:, 64:192], ent + ["nq%d" % b], ["pd%d" % b], False, True)
        for c in range(4):
            ts(off[:, c:c + 1], T.pyk[:, 20 + c:21 + c], T.ppl[:, c:c + 1], T.islot[:, c:c + 1], A.min, A.max, ["pyk", "ppl", "islot"], ["off%d_%d" % (h, c)])
        offs = ["off%d_%d" % (h, c) for c in range(4)]
        for (a, b, i) in ((0, 2, "_"), (2, 4, "")):
            cp(p[:, 16 * a:16 * b].bitcast(dt.uint32), w[:, 0:Z0].bitcast(dt.uint32).indirect(off[:, a:b]), offs[a:b] + pan, ["p%s%d" % (i, h)])
            act(q[:, 16 * a:16 * b], v[:, 0:Z0].indirect(off[:, a:b]), F.Copy, offs[a:b] + pan, ["q%s%d" % (i, h)])
        pqs = [c + i + "%d" % h for c in "pq" for i in ("_", "")]
        if h < H:
            send(h)
        cp(win[:].indirect(off[:, 0:4]), T.vals[:], offs + ["vals", "win%d" % h], ["win%d" % h])
        if h == 1:
            ts(T.dcol[:], T.i6b[:, 0:1], 15.0, 2.0 ** -10, A.is_ge, A.max, ["i6b"], ["dcol"])
        for b in range(4):
            act(T.zt[:, b:256:4], T["pd%d" % b][:, 0:P], F.Copy, ["pd%d" % b], ["zt%d" % b])
        scan(T.scn[:], T.seg[:], win[:, T0:Z0], 0.0, A.mult, A.max, ["seg", "win%d" % h], ["scn"])
        if h == 1:
            quant(T.wq[:], T.ws[:], T.tw[:], ["tw"], ["wq"])
        quant(w[:, Z0:E0], v[:, Z0:E0], T.zt[:], ["zt0", "zt1", "zt2", "zt3", "zzt256", "zzt384"], ["wz%d" % h])
        ts(tof[:], T.scn[:, 15:C:16], T.dcol[:], -1.0, A.mult, A.add, ["scn", "dcol"], ["tof%d" % h])
        mm(T.pyk[:, 0:128], T.wq[:], T.ws[:], p[:, 0:128], q[:, 0:128], pqs + ent + ["wq"], ["pyk"])
        act(T.ys[:, (h - 1) * P:h * P], T.pyk[:, 0:P], F.Copy, ["pyk"], ["ys%d" % h])
        tab = [wb, vb, "wz%d" % h, "tof%d" % h]
        for (a, b, i) in (((0, 6, "_"), (6, 12, "")) if h == H else ((0, 12, ""),)):
            l, r = T0 + 16 * a, T0 + 16 * b
            cp(w2[:, l:r].bitcast(dt.uint32), w[:, T0:E0].bitcast(dt.uint32).indirect(tof[:, a:b]), tab, ["wb%s%d" % (i, h + 1)])
            act(v2[:, l:r], v[:, T0:E0].indirect(tof[:, a:b]), F.Copy, tab, ["vb%s%d" % (i, h + 1)])
        if h == 1: urep(2)
        if h < H:
            pad(h + 1)
            if h + 2 <= H: urep(h + 2)
        if h == 1:
            for k in range(2, H + 1):
                iota(T["win%d" % k][:, T0:Z0], [[1, C]], 1, 0, "win%d" % k)
        if h == H:
            dma("Y", T.pc[:], p[:, 0:P].bitcast(dt.uint8), "fin", ["p%d" % h, "p_%d" % h], [])
            for k in range(4):
                dma("Y", T.psc[4 * k:4 * k + 4, :], q[32 * k:32 * k + 4, 0:P], "fin", ["q%d" % h, "q_%d" % h], [])
        dma("Y", T.y[:, (h - 1) * P:h * P], T.ys[:, (h - 1) * P:h * P], "st%d" % h, ["ys%d" % h], [])
    e = H + 1
    for (a, b, i) in ((0, 6, "_"), (6, 12, "")):
        dma("Y", T.oc[:, 64 * a:64 * b], T["w%d" % e][:, T0 + 16 * a:T0 + 16 * b].bitcast(dt.uint8), "fin", ["wb%s%d" % (i, e)], [])
    for k in range(4):
        dma("S" if k % 2 else "Y", T.osc[4 * k:4 * k + 4, :], T["v%d" % e][32 * k:32 * k + 4, T0:Z0], "fin", ["vb_%d" % e, "vb%d" % e], [])
    for sem in sorted(last):
        need("G", (sem, last[sem], {}))
